import numpy as np, ml_dtypes
CORES = [3,11,19,27,35,43,51,59]
N = 8
BF = ml_dtypes.bfloat16
W, I, S, JU, RO = 3072, 1024, 4, 4, 2
def pick(a, ix):
    return np.take_along_axis(a, ix, 2) if a.ndim == 3 else np.take_along_axis(a, ix[:, :, None, :], 3)
def walk(u, par, side, heads):
    w = heads; c = heads; acc = np.zeros((N, 8, 16, I), np.int64)
    for _ in range(S):
        v = pick(u, w); up = np.add.reduce((v >= 4).astype(np.int64), axis=2) >= 9
        acc = acc + np.where(up[:, :, None, :], v, 0)
        sd = pick(side, c); w = np.where(up, pick(par, w), sd); c = np.where(up, c, sd)
    return acc
def forest(rng, alike, noise, ex):
    par = np.zeros((N, 8, W), np.int64); side = np.zeros((N, 8, W), np.int64); itm = np.zeros((N, 8, W), np.int64); bit = np.zeros((N, 8, W), np.int64); heads = np.zeros((N, 8, I), np.int64)
    pop = [rng.permutation(I) for g in range(8)]; n = np.arange(W); m = np.arange(W - 1)
    for q in range(N):
        for g in range(8):
            it = pop[g][np.minimum((I * rng.random(W) ** ex).astype(np.int64), I - 1)]; itm[q, g] = it
            o = np.argsort(it[1:], kind="stable") + 1; k = it[o]
            new = np.concatenate([np.array([True]), k[1:] != k[:-1]])
            side[q, g, o[:-1]] = np.where(new[1:], 0, o[1:]); heads[q, g, k[new]] = o[new]
            base = np.maximum(np.minimum((n * rng.random(W) ** 0.4).astype(np.int64), n - 1), 0)
            run = np.maximum.accumulate(np.where(new | (rng.random(W - 1) >= alike), m, 0))
            par[q, g, o] = base[o[run]]
            bit[q, g, o] = (m + (rng.random(W - 1) < noise)) & 1
    return par, side, itm, bit, heads
def counts(rng, e):
    lev = rng.random((N, 8, 1, W)) ** e
    u = np.where(rng.random((N, 8, 16, W)) < lev, rng.integers(4, 16, (N, 8, 16, W)), rng.integers(0, 4, (N, 8, 16, W)))
    u[..., 0] = 0
    return u
def level(u, par, side, heads, share):
    s = np.sort(np.add.reduce(walk(u, par, side, heads), axis=0), axis=2)
    j = np.minimum((I * share).astype(np.int64), I - 1)
    return np.clip(s[np.arange(8)[:, None], np.arange(16)[None, :], j[:, None]], 1, 1024)
def pack(u, par, side, itm, bit, heads, th):
    return {"cnt": np.ascontiguousarray(u.reshape(N, 128, W)).astype(np.float32).astype(BF), "par": par.astype(np.int32), "side": side.astype(np.int32), "itm": itm.astype(np.int32),
            "bit": bit.astype(np.int32), "heads": heads.astype(np.int32), "th": np.repeat(th.reshape(1, 128, 1), N, axis=0).astype(np.int32)}
def setup_inputs(rng):
    par, side, itm, bit, heads = forest(rng, 0.5, 0.25, 2.0); u = counts(rng, 0.5)
    return pack(u, par, side, itm, bit, heads, level(u, par, side, heads, 0.35 + 0.4 * rng.random(8)))
def setup_inputs_ties(rng):
    par, side, itm, bit, heads = forest(rng, 0.5, 0.25, 2.0)
    r = np.argsort(rng.random((N, 8, 16, W)), axis=2); m = 8 + (rng.random((N, 8, 1, W)) < 0.7)
    u = np.where(r < m, np.where(rng.random(r.shape) < 0.8, 4, rng.integers(4, 16, r.shape)), 3); u[..., 0] = 0
    tot = np.add.reduce(walk(u, par, side, heads), axis=0)
    i0 = np.argsort(np.min(tot, axis=1), axis=1, kind="stable")[:, I // 2]
    x = np.stack([tot[g, :, i0[g]] for g in range(8)]); k = np.argsort(rng.random((8, 16)), axis=1)
    th = np.where(k < 8 + (np.arange(8)[:, None] & 1), x, x + 1)
    return pack(u, par, side, itm, bit, heads, np.clip(th, 1, 1024))
def setup_inputs_deep(rng):
    par, side, itm, bit, heads = forest(rng, 0.5, 0.25, 2.0); u = counts(rng, 0.5); n = np.arange(W)
    par[:, 0::2] = np.maximum(n - 1, 0); par[:, 1::2] = np.maximum(n - 1 - rng.integers(0, 3, (N, 4, W)), 0)
    u = np.where(rng.random((N, 8, 1, W)) < 0.15, 15, u); u[..., 0] = 0
    th = level(u, par, side, heads, np.array([0.8, 0.9, 0.7, 0.5, 0.5, 0.5, 0.95, 0.6]))
    th[3] = 1024; th[4] = 1
    return pack(u, par, side, itm, bit, heads, th)
def one_chain(rng, par, side, itm, bit, heads, u):
    for q in range(N):
        for g in range(4):
            o = np.concatenate([np.array([W - 1]), rng.permutation(W - 2) + 1]); top = o[1]
            side[q, g] = 0; side[q, g, o[:-1]] = o[1:]
            if g == 1: side[q, g, o[1::2]] = 0
            bit[q, g, o] = (np.arange(W - 1) + (g == 1)) & 1
            par[q, g] = top; par[q, g, 0] = 0
            itm[q, g] = rng.integers(0, I, W); itm[q, g, top] = 0
            heads[q, g] = rng.integers(1, W, I); heads[q, g, 0] = top
            u[q, g] = rng.integers(4, 16, (16, W)); u[q, g, :, top] = rng.integers(12, 16, 16); u[q, g, :, 0] = 0
def setup_inputs_merge(rng):
    par, side, itm, bit, heads = forest(rng, 0.9, 0.5, 3.0); u = counts(rng, 0.4)
    one_chain(rng, par, side, itm, bit, heads, u)
    th = level(u, par, side, heads, 0.03 + 0.17 * rng.random(8))
    tot = np.add.reduce(walk(u, par, side, heads), axis=0)
    th[:2] = np.min(tot[:2], axis=2)
    th[2] = np.sort(tot[2], axis=1)[:, I // 2] | 1
    i0 = np.argsort(np.add.reduce(tot[3], axis=0), kind="stable")[I // 2]; k = np.argsort(rng.random(16))
    th[3] = np.where(k < 9, tot[3, :, i0], tot[3, :, i0] + 1)
    return pack(u, par, side, itm, bit, heads, th)
def setup_inputs_wild(rng):
    par = rng.integers(0, W, (N, 8, W)); itm = rng.integers(0, I, (N, 8, W)); bit = rng.integers(0, 2, (N, 8, W)); side = np.zeros((N, 8, W), np.int64)
    par[..., 1] = W - 1; zz = np.zeros((N, 8), np.int64)
    for q in range(N):
        for g in range(8):
            o = rng.permutation(W - 1) + 1; x, y, z, rest = o[:32], o[32:64], o[64], o[65:]
            a, b = rng.permutation(rest), rng.permutation(rest); h = W - W // 5
            side[q, g, a[:h]] = b[:h]; side[q, g, x] = y; side[q, g, y] = x; side[q, g, z] = z; zz[q, g] = z; bit[q, g, x] = 0; bit[q, g, y] = 1
            sel = np.nonzero((side[q, g] > 0) & (rng.random(W) < 0.6))[0]; p = par[q, g].copy(); p[side[q, g, sel]] = par[q, g, sel]; p[y] = p[x]; p[z] = 0; par[q, g] = p
    par[..., 0] = 0
    heads = np.where(rng.random((N, 8, I)) < 0.3, rng.choice(np.array([0, 1, W - 1]), (N, 8, I)), rng.integers(0, W, (N, 8, I)))
    heads[:, 0] = rng.choice(np.array([1, W - 1, W // 2, 5]), (N, I))
    heads[:, :, 3] = zz
    u = counts(rng, 0.5); u[np.arange(N)[:, None], np.arange(8)[None, :], :, zz] = 15
    return pack(u, par, side, itm, bit, heads, level(u, par, side, heads, 0.3 + 0.3 * rng.random(8)))
def setup_inputs_spread(rng):
    par, side, itm, bit, heads = forest(rng, rng.random(), 0.3, 4.0)
    u = np.minimum((16 * rng.random((N, 8, 16, W)) ** np.exp2(rng.integers(-3, 3, (N, 8, 1, W)))).astype(np.int64), 15)
    u = np.where(rng.random((N, 8, 1, W)) < 0.0625, 0, u); u[..., 0] = 0
    return pack(u, par, side, itm, bit, heads, level(u, par, side, heads, rng.permutation(np.array([0.02, 0.15, 0.3, 0.45, 0.55, 0.7, 0.85, 0.97]))))
def check_inputs(d):
    bad = []
    for k, lo, hi in (("par", 0, W - 1), ("side", 0, W - 1), ("itm", 0, I - 1), ("bit", 0, 1), ("heads", 0, W - 1), ("th", 1, 1024)):
        if np.min(d[k]) < lo or np.max(d[k]) > hi: bad.append("range of " + k)
    c = d["cnt"].astype(np.float32)
    if not np.all((c >= 0) & (c <= 15) & (c == np.floor(c))): bad.append("cnt: whole numbers from 0 to 15")
    if np.any(c[:, :, 0] != 0): bad.append("cnt of node 0")
    for k in ("par", "side"):
        if np.any(d[k][:, :, 0] != 0): bad.append(k + " of node 0")
    s = np.sort(d["side"], axis=2)
    if np.any((s[:, :, 1:] == s[:, :, :-1]) & (s[:, :, 1:] != 0)): bad.append("side: numbers other than 0 differ")
    if np.any(d["th"] != d["th"][:1]): bad.append("th alike on all ranks")
    return bad
def reference(cnt, par, side, itm, bit, heads, th):
    u = cnt.astype(np.float32).astype(np.int64).reshape(N, 8, 16, W); pa = par.astype(np.int64); sd = side.astype(np.int64)
    it = itm.astype(np.int64); b = bit.astype(np.int64); hd = heads.astype(np.int64); lim = th[0].astype(np.int64).reshape(8, 16, 1)
    node = np.broadcast_to(np.arange(W), (N, 8, W)); own = []
    for t in range(RO):
        tot = np.add.reduce(walk(u, pa, sd, hd), axis=0)
        own.append(np.stack([tot[:, :, r * (I // N):(r + 1) * (I // N)].reshape(128, I // N) for r in range(N)]))
        kept = np.add.reduce((tot >= lim).astype(np.int64), axis=1) >= 9
        kn = pick(np.broadcast_to(kept[None], (N, 8, I)), it); kn[:, :, 0] = True
        jump = np.where(kn, node, pa); p1 = pa
        for _ in range(JU): p1 = pick(jump, p1)
        u1 = np.where(pick(kn, pa)[:, :, None, :], u, np.minimum(15, u + pick(u, pa)))
        ab = kn & (sd != 0) & (p1 == pick(p1, sd)) & (b == t % 2) & (pick(b, sd) == 1 - t % 2)
        u = np.where(ab[:, :, None, :], np.minimum(15, u1 + pick(u1, sd)), u1)
        rep = np.array(node); a, g, n = np.nonzero(ab); rep[a, g, sd[a, g, n]] = n
        sd = np.where(ab, pick(sd, sd), np.where(rep != node, 0, sd))
        pa = pick(rep, p1)
    return {"ya": np.concatenate(own, axis=2).astype(np.float32), "yc": np.ascontiguousarray(u.reshape(N, 128, W)).astype(np.float32).astype(BF), "yp": pa.astype(np.float32)}

@@ -1,0 +1,585 @@
+from concourse.bass import DstId, RemoteDMATransfer
+from concourse.mybir import AluOpType as ALU, ActivationFunctionType as AF
+
+W, M, I, MI = 3072, 192, 1024, 64
+BF, F, I32, U16 = "bfloat16", "float32", "int32", "uint16"
+NX, SD, JJ, FL, ID, DL, PA, IT = 0, 2, 4, 6, 7, 9, 11, 13
+WV = {"vv": None, "pa": {11: 1, 12: 1}, "sd": {2: 1, 3: 1}, "nx": {0: 1, 1: 1}, "sg": {7: 1, 8: 16},
+      "jj": {4: 1, 5: 1}, "mf": {4: 1, 5: 1, 6: 4096}, "md": {4: -1, 5: -1, 6: 12288},
+      "rp": {7: 192, 8: 1, 9: 192, 10: 1}, "rq": {7: 1}, "rm": {8: 1},
+      "it": {13: 1, 14: 1}, "kp": {0: 8192}, "kn": {0: 16384}}
+WOFF = {k: 144 * i for i, k in enumerate(WV)}
+
+SCRATCH = {}
+
+
+def _sb(names, cols, dty):
+    for n in names.split():
+        SCRATCH[n] = ("sbuf", [128, cols], dty)
+
+
+_sb("tab", 3 * W, BF)
+_sb("pt", 2 * W, BF)
+_sb("att us ua ub ge ga gb gc2 gd gf", W, BF)
+_sb("un", W + 16, BF)
+_sb("wv", 144 * len(WV), BF)
+_sb("idn id3 bo ones gev", 128, BF)
+_sb("kt0 kt1", I + 16, BF)
+_sb("snd0 snd1 lnd0 lnd1 gw0 gw1 gu0 gu1 gu2 gu3", I, BF)
+_sb("yas", 256, F)
+_sb("pai sdi iti bti x3 xj xk", M, I32)
+_sb("hdi", MI, I32)
+_sb("thi pi", 4, I32)
+_sb("col", 8, F)
+_sb("mf nf sf3 paf pa3 sdf sd1 btf itf p2f t1 t2 t3 t4 t5 t6 t7 xx nx0 th0 th1 sgs d2 ma mb tj ypf", M, F)
+_sb("pah pal sdh sdl ith itl idq idm nh nl one twos ro0 ro1 eb jh jl dq dm deh del n0h n0l n1h n1l", M, BF)
+_sb("opa osd oit oip opm od oi op0 op1 osm osc", M, U16)
+_sb("ow om", 4 * MI, U16)
+_sb("osh", MI, U16)
+_sb("hdf h3 hs hx", MI, F)
+_sb("wf nf3 sck sc wn wm", 4 * MI, F)
+for _b in range(8):
+    SCRATCH["ps%d" % _b] = ("psum", [128, 512], F)
+
+NDMA = 72
+SEMAPHORES = ["cv", "ca", "cp", "cg", "rs0", "rs1", "kv0", "kv1", "loc"] + ["d%d" % i for i in range(NDMA)]
+
+CY, PCY, GA, SC, FIX, HOP = 1.04e-3, 0.5e-3, 1.56, 3.8, 0.06, 0.15
+DMAL, REML = 2.3, 5.5
+TTU = True
+ORDER = """
+9a es 11v 37g ca fs 0a 2s 1a 3s ba 10s 5s 7a 4s aa 8a 6a da 44v 13g 14g 1ag 4fa 4bv 18g 4av 1bg 12v 3cv 5ds 19g 52v 36g 97a 53v 54a 15v 3dv 5ea 55v 58s 56a 94a 6dv 5as 59s 9aa 99a 47v 6bv 3fa 16g 3ea 49v 6fa 17g 61v 1eg 57v 6cp 3ag 4ev 71a 5bs 6ep 62v a3v 5cs 45v 70p 9da 9ca 72p 9fa 30g 95a 32g a2a 39g 73v 96a 5fs 60s 40v 98a 74v 42a 63a 46v 64a 38g 7fv a1a 65p 8av 77a 35v 75a 89v 7bs 67p a4a 8bv 79s 43v 1cg 76v 1fg 33g a5a 4cv 69p 7as 78v 3bg 88v 82a 7cs a6p 6av 68a 8cv 9ea 41a 48v 66a 83a 8dv 81a 2eg a7v 80a eas 8ev 2dg a9v 2cg 8fa aav 1dg a8v a0a acv 25g 92s 50a 90v 20g 2fg b3a 21g b2v 28g 93s 29g 9ba 2ag 87v b0a 85v b4p adv 2bg abv 31g 84v 22g b5v 7dv 23g b1p c1a b6v 26g c2v b8p 24g 27g 34g aea b7v b9v c3p bbv bav bfa bcv afp 86v 91v f9p 4dv c4v bda cdv cea c5v c0p c6v bep c7v eba fav cfp e9s e7s c8v e8s fbv cba d0v fcv d1v c9v d4a ccp fdv cap d2a d5p d7a d3p fev d6a eda d8g ffv efa 100v eca 101v eea f1p f5p f0a 7ev 102v f6p 109a f7p 103v 10ea f2p 10aa 51v d9p f8v dav 10ca dbp dev f3p dcv 104v ddg 10da 113p 10fp e5v dfa e2a 105v e0a e3a e4a 10ba e1v 106v e6a 114p 115p f4v 107v 110p 111p 108v 112a 117p 120a 124v 121v 12ba 122v 123a 126p 125v 12da 127p 116v 12ea 128p 12cv 130a 137p 118v 129v 131p 12fa 138v 13av 12av 132v 13bv 134v 13dp 13cv 135v 133v 136v 11cp 13ev 139v 140v 13fv 141v 142v 145s 143s 119v 147s 144s 146s 148s 11ep 11dv 14av 149v 152a 14cv 14fa 150v 151a 11av 155p 14bv 153a 157p 156v 14dv 154a 11fv 15ba 14ev 159p 15ca 158v 15av 15dv 15ea 16bp 15fv 161p 160a 172p 11bv 179p 165a 166v 169a 16av 16cp 167a 16dv 17ap 16ev 171v 162p 17bv 168a 17cv 17dv 17fv 191v 190a 173p 163p 17ev 194a 170v 174v 16fv 175v 176v 195a 178v 180s 177v 182v 181s 183v 193a 184v 185v 192a 164v 186v 189v 196p 187a 1b2a 197p 188v 18as 1a7p 199p 1b4v 18bs 19dp 1b6a 19ap 19ep 198v 1a4p 1b3a 1abp 19fv 1a5p 1a0p 19bv 1a8p 21ba 1acp 21ev 21aa 1bep 21cv 1a9v 18ca 1a1p 18dv 1b5a 1a6v 18ep 1a2v 1b7a 1bfp 18fv 19cv 1aep 1adv 1b8s 1bba 1afp 1b9s 1c3p 1a3v 1c0p 1b0v 1baa 1aav 1c4p 227v 225a 1c5p 1b1v 1c1a 224v 1c2a 1c6p 226v 228v 1d6a 1d1v 1bcp 1c7v 1c8v 1cba 1d2a 1ccv 1cfs 1c9a 1d4s 1d7a 1bdv 1cds 1cav 1d0s 223v 1ces 1d3v 229a 1d8p 222a 21dv 221a 1d5s 220v 21fa 1d9v 1dcv 1dev 1dav 1e0a 1dbv 1dfv 1ddv 1e4v 1e5a 1e1p 22bv 22fa 1e6p 1eap 1e7v 1e8v 1f4a 1f3v 1e2a 1e9v 1ebv 1f5p 1edv 1ecv 1eev 1efa 1f6v 1e3p 1f7v 1f8v 200v 1ffa 1f0p 1f9v 1f1a 1fav 201p 1fdv 1fba 1f2p 202v 203v 1fep 204a 206v 1fcp 22ea 207p 205p 209v 208a 22av 22da 20ag 234p 22ca 230p 235p 231p 236p 232p 237v 233v 20bp 20cv 20dp 210a 20ev 216a 215v 217a 218v 211a 20fg 212a 213a 214a 219s 238a 23dv 239a 23av 23bv 23ca 23ep 243a 244v 23fp 245v 246a 240p 249p 241v 248a 247v 24fp 24av 250v 255p 24bv 24cv 242v 24dv 256v 252v 258v 257v 259v 253v 25av 25ds 254v 25bs 25fs 24ev 261v 25cs 260s 25es 262v 251v 267a 268v 26bv 26ca 26dp 26aa 26ev 271p 269v 274a 272v 266v 26fp 278a 270v 273v 276a 275v 279p 277a 283p 264v 27ap 27ea 28ap 263v 27da 27bp 265v 291p 281a 284p 280v 27fa 285v 27cv 282a 286v 28bp 289v 287v 288v 29aa 28cv 292p 28fv 28dv 28ev 293v 29ba 294v 295v 296v 298s 290v 299s 297v 29ea 29fv 29cv 29da 2a7p 2bca 2bfv 2b8p 2a8p 2a0p 2aap 2a9v 2bda 2a3p 2b9p 2a1p 2bav 2aep 2c1a 2b1p 2a2v 2b5p 2a4p 2abp 2bea 2a5v 2b2p 2c2p 2acv 2a6s 2c0a 2b6p 2b3v 2ads 2afp 2b7v 2c3p 2b0v 2bbs 2c4p 2b4s 2c5v 2c6s
+"""
+
+
+def build(g, T, topo, core, rank):
+    ops = []
+    log = {}
+    N = len(T.cores)
+
+    def A(name, c0=0, c1=None, step=1, row=None):
+        if c1 is None:
+            c1 = SCRATCH[name][1][1]
+        if row is not None:
+            ap = T[name][row::16, c0:c1]
+        elif step != 1:
+            ap = T[name][:, c0:c1:step]
+        else:
+            ap = T[name][:, c0:c1]
+        return (ap, name, c0, c1, row, len(range(c0, c1, step)), step)
+
+    def two(*a):
+        return all(SCRATCH[x[1]][2] in (BF, U16) for x in a)
+
+    def op(engs, dur, fn, R, Wr, lat=0.0, kind="c", ext=()):
+        k = len(ops)
+        deps = {}
+        for acc, wr in ((R, False), (Wr, True)):
+            for a in acc:
+                name, c0, c1, row, st = a[1], a[2], a[3], a[4], a[6]
+                psum = name.startswith("ps")
+                if psum:
+                    c0, c1, st = 0, 512, 1
+                lst = log.setdefault(name, [])
+                for (j, d0, d1, drow, dwr, dst_) in lst:
+                    if j == k or d1 <= c0 or c1 <= d0 or (row is not None and drow is not None and row != drow):
+                        continue
+                    if st > 1 and st == dst_ and (c0 - d0) % st:
+                        continue
+                    if dwr or wr:
+                        deps[j] = True
+                    elif psum:
+                        deps.setdefault(j, False)
+                if wr and row is None and st == 1:
+                    lst[:] = [e for e in lst if not (c0 <= e[1] and e[2] <= c1)]
+                lst.append((k, c0, c1, row, wr, st))
+        for j in ext:
+            deps[j] = True
+        if not isinstance(dur, dict):
+            dur = {e: dur for e in engs}
+        ops.append({"engs": engs, "dur": dur, "fn": fn, "deps": deps, "lat": lat, "kind": kind, "tag": (Wr or R)[0][1]})
+        return k
+
+    def sc_ap(s):
+        return s[0] if isinstance(s, tuple) else s
+
+    def ts(out, in0, s1, s2, op0, op1=None):
+        rd = [in0] + [s for s in (s1, s2) if isinstance(s, tuple)]
+        d = FIX + CY * max(64, out[5] * (0.5 if two(out, in0) else 1))
+        if op1 is None:
+            fn = lambda e: g.vector.tensor_scalar(out[0], in0[0], sc_ap(s1), None, op0)
+        else:
+            fn = lambda e: g.vector.tensor_scalar(out[0], in0[0], sc_ap(s1), sc_ap(s2), op0, op1)
+        return op("v", d, fn, rd, [out])
+
+    def tt(out, a, b, alu):
+        ps = a[1].startswith("ps") or b[1].startswith("ps")
+        d = FIX + CY * max(64, out[5] * (1 if ps else 2))
+        return op("v", d, lambda e: g.vector.tensor_tensor(out[0], a[0], b[0], alu), [a, b], [out])
+
+    def ttu(out, tmp, a, b, alu):
+        if TTU:
+            return tt(out, a, b, alu)
+        tt(tmp, a, b, alu)
+        return aff(out, tmp)
+
+    def aff(out, in0, mul=1.0, add=0.0):
+        fl = all(SCRATCH[x[1]][2] in (BF, F) for x in (out, in0))
+        plain = mul == 1.0 and add == 0.0
+
+        def fn(e):
+            if e == "a":
+                if plain:
+                    return g.scalar.activation(out[0], in0[0], AF.Copy)
+                return g.scalar.activation(out[0], in0[0], AF.Identity, bias=float(add), scale=float(mul))
+            if plain:
+                return g.vector.tensor_copy(out[0], in0[0])
+            return g.vector.tensor_scalar(out[0], in0[0], float(mul), float(add), ALU.mult, ALU.add)
+        d = {"v": FIX + CY * max(64, out[5] * (0.5 if two(out, in0) else 1)), "a": FIX + CY * max(64, out[5])}
+        return op("va" if fl else "v", d, fn, [in0], [out])
+
+    def relu(out, in0):
+        def fn(e):
+            if e == "a":
+                return g.scalar.activation(out[0], in0[0], AF.Relu)
+            return g.vector.tensor_scalar(out[0], in0[0], 0.0, None, ALU.max)
+        return op("va", FIX + CY * max(64, out[5]), fn, [in0], [out])
+
+    def ge4(out, in0):
+        def fn(e):
+            if e == "a":
+                return g.scalar.activation(out[0], in0[0], AF.Sign, bias=-3.5)
+            return g.vector.tensor_scalar(out[0], in0[0], 4.0, 0.5, ALU.is_ge, ALU.subtract)
+        return op("va", {"v": FIX + CY * out[5] * 0.5, "a": FIX + CY * out[5]}, fn, [in0], [out])
+
+    def mset(out, val):
+        d = FIX + CY * max(64, out[5] * (0.5 if two(out) else 1))
+        return op("v", d, lambda e: g.vector.memset(out[0], val), [], [out])
+
+    def gather(out, win, off, k0, k1, add=None, ext=()):
+        o, f = A(out, 16 * k0, 16 * k1), A(off[0], off[1] + k0, off[1] + k1)
+        d = FIX + CY * GA * o[5]
+        if add is None:
+            def fn(e):
+                if e == "a":
+                    return g.scalar.activation(o[0], win[0].indirect(f[0]), AF.Copy)
+                return g.vector.tensor_copy(o[0], win[0].indirect(f[0]))
+            return op("va", d, fn, [win, f], [o], ext=ext)
+        b = A(add, 16 * k0, 16 * k1)
+        return op("v", d * 1.1, lambda e: g.vector.tensor_tensor(o[0], win[0].indirect(f[0]), b[0], ALU.add), [win, f, b], [o])
+
+    def mm(out, terms, start=True, stop=True, ext=()):
+        def fn(e):
+            ins = None
+            for i, (l, r) in enumerate(terms):
+                ins = g.tensor.matmul(out[0], l[0], r[0], start and i == 0, stop and i == len(terms) - 1)
+            return ins
+        d = 0.05 + PCY * sum(max(64, r[5]) for l, r in terms)
+        return op("p", d, fn, [x for t in terms for x in t], [out], ext=ext)
+
+    def wq(v, q):
+        return A("wv", WOFF[v] + 15 - q, WOFF[v] + 143 - q)
+
+    def sig(v, buf, j):
+        return [(wq(v, q), A(buf, 1024 * j + q, 1024 * (j + 1), 16)) for q in range(16)]
+
+    def nat(v, buf, qs=range(16)):
+        return [(wq(v, q), A(buf, M * q, M * (q + 1))) for q in qs]
+
+    nb = [0, 6]
+
+    def bank(n=64):
+        b = nb[0] % nb[1]
+        nb[0] += 1
+        return A("ps%d" % b, 0, n)
+
+    def fold(terms, n=64):
+        b = bank(n)
+        mm(b, terms)
+        return b
+
+    def whole(v, buf):
+        b = bank(M)
+        for j in range(3):
+            mm(A(b[1], 64 * j, 64 * j + 64), sig(v, buf, j))
+        return b
+
+    def dma(out, in_, R, Wr, q="s", lat=DMAL):
+        fn = lambda e: (g.sync if e == "s" else g.scalar).dma_start(out, in_)
+        return op(q, 0.1, fn, R, Wr, lat=lat, kind="d")
+
+    def torow(tabn, row, c0, src):
+        o = A(tabn, c0, c0 + W, row=row)
+        return dma(o[0], T[src][:], [A(src)], [o])
+
+    def digits(h, l, x, c0=0, c1=M):
+        aff(A(h, c0, c1), A(x, c0, c1))
+        tt(A(l, c0, c1), A(x, c0, c1), A(h, c0, c1), ALU.subtract)
+
+    def gp(dur, fn, R, Wr):
+        return op("g", dur, fn, R, Wr)
+
+    def CH(name, j):
+        return A(name, 64 * j, 64 * j + 64)
+
+    def g6(out, win, off, add=None, ext=()):
+        for c in range(6):
+            gather(out, win, (off, 0), 32 * c, 32 * c + 32, add, ext)
+
+    def g2(out, win, off, c0=0):
+        for h in range(2):
+            gather(out, win, (off, c0), 32 * h, 32 * h + 32)
+
+    for nm, src in (("pai", T.par), ("sdi", T.side)):
+        dma(T[nm][:], src[:], [], [A(nm)], q="a", lat=2.4)
+    for j in range(4):
+        a = A("un", 768 * j, 768 * (j + 1))
+        dma(a[0], T.cnt[:, 768 * j:768 * (j + 1)], [], [a], q="s", lat=3.0 + 0.9 * j)
+    for r in range(N):
+        a = A("hdi", 8 * r, 8 * r + 8)
+        dma(a[0], T.heads[:, 128 * r:128 * (r + 1)], [], [a], q="a", lat=3.5)
+    for nm, src in (("bti", T.bit), ("iti", T.itm)):
+        dma(T[nm][:], src[:], [], [A(nm)], q="s", lat=5.0)
+    dma(T.thi[:, 0:1], T.th[:], [], [A("thi")], q="s", lat=5.0)
+
+    mset(A("wv"), 0.0)
+    mset(A("ones"), 1.0)
+    gp(0.2, lambda e: g.iota(T.pi[:, 0:1], [[0, 1]], 0, 1), [], [A("pi", 0, 1)])
+    gp(0.5, lambda e: g.iota(T.mf[:], [[1, M]], 0, 0, allow_small_or_imprecise_dtypes=True), [], [A("mf")])
+    for v, rows in WV.items():
+        a = A("wv", WOFF[v] + 15, WOFF[v] + 143, 16)
+        if rows is None:
+            mset(a, 16384.0)
+            gp(0.2, lambda e, a=a: g.affine_select(a[0], a[0], [[-16, 8]], ALU.is_ge, 0.0, 0, 1), [a], [a])
+            gp(0.2, lambda e, a=a: g.affine_select(a[0], a[0], [[16, 8]], ALU.is_ge, 0.0, 15, -1), [a], [a])
+        else:
+            for r, w in rows.items():
+                gp(0.2, lambda e, a=a, r=r, w=w: g.affine_select(a[0], a[0], [[-16, 8]], ALU.not_equal, float(w), -r, 1), [a], [a])
+    gp(0.4, lambda e: g.affine_select(T.idn[:], T.ones[:], [[-1, 128]], ALU.is_equal, 0.0, 0, 1), [A("ones")], [A("idn")])
+    gp(0.4, lambda e: g.affine_select(T.bo[:], T.ones[:], [[-16, 8], [0, 16]], ALU.is_ge, 0.0, 0, 1), [A("ones")], [A("bo")])
+    gp(0.4, lambda e: g.affine_select(T.bo[:], T.bo[:], [[16, 8], [0, 16]], ALU.is_ge, 0.0, 15, -1), [A("bo")], [A("bo")])
+    aff(A("id3"), A("idn"), 3072.0)
+    for nm, c0 in (("pt", 0), ("tab", 2 * W)):
+        for c in range(3):
+            a = A(nm, c0 + I * c, c0 + I * (c + 1))
+            gp(1.9, lambda e, a=a: g.iota(a[0], [[0, I]], 0, 0, allow_small_or_imprecise_dtypes=True), [], [a])
+    ts(A("pi", 1, 2), A("pi", 0, 1), 15, None, ALU.bitwise_and)
+    cq, cq192, cnz, cz, cth, cb, cq3 = [A("col", i, i + 1) for i in range(7)]
+    aff(cq, A("pi", 1, 2))
+    aff(cq192, cq, 192.0)
+    aff(cq3, cq, 1.0, 3072.0)
+    ts(cnz, cq, 0.5, None, ALU.is_ge)
+    aff(cz, cnz, -1024.0, 1024.0)
+    aff(cb, cnz, -1e6, 1e6)
+    aff(cth, A("thi", 0, 1))
+    mset(A("att"), 0.0)
+    mset(A("tab", 0, W), 0.0)
+    mset(A("tab", W, 2 * W), 0.0)
+    mset(A("un", W, W + 16), 0.0)
+    mset(A("one"), 1.0)
+    mset(A("twos"), 2.0)
+    for t in range(2):
+        mset(A("kt%d" % t, I, I + 16), 0.5)
+    ts(A("nf"), A("mf"), cq192, None, ALU.add)
+    ts(A("sf3"), A("mf"), 16.0, cq3, ALU.mult, ALU.add)
+    ts(A("idq"), A("mf"), 0.0, cq, ALU.mult, ALU.add)
+    aff(A("idm"), A("mf"))
+    digits("nh", "nl", "nf")
+
+    aff(A("paf"), A("pai"))
+    aff(A("sdf"), A("sdi"))
+    digits("pah", "pal", "paf")
+    digits("sdh", "sdl", "sdf")
+    for row, src in ((PA, "pah"), (PA + 1, "pal"), (SD, "sdh"), (SD + 1, "sdl"), (ID, "idq"), (ID + 1, "idm")):
+        torow("att", row, 0, src)
+    aff(A("pa3"), A("paf"), 1.0, 3072.0)
+    torow("tab", SD, 0, "sdh")
+    torow("tab", SD + 1, 0, "sdl")
+    aff(A("ow", 0, MI), A("hdi"))
+    aff(A("hdf"), A("hdi"))
+    g2("gu1", A("att"), "ow")
+    aff(A("h3"), fold(sig("pa", "gu1", 0)), 1.0, 3072.0)
+    aff(A("hs"), fold(sig("sd", "gu1", 0)))
+    aff(A("osh"), fold(sig("sg", "gu1", 0)))
+
+    def nxt(pv, sdn):
+        tt(A("xx"), pv, A("pa3"), ALU.min)
+        tt(A("nx0"), A("xx"), A(sdn), ALU.max)
+        digits("n0h", "n0l", "nx0")
+        digits("n1h", "n1l", "xx")
+        torow("tab", NX, 0, "n0h")
+        torow("tab", NX + 1, 0, "n0l")
+        torow("tab", NX, W, "n1h")
+        torow("tab", NX + 1, W, "n1l")
+
+    pv = bank(M)
+    for j in range(4):
+        ge4(A("ge", 768 * j, 768 * (j + 1)), A("un", 768 * j, 768 * (j + 1)))
+        mm(pv, nat("vv", "ge", range(4 * j, 4 * j + 4)), j == 0, j == 3)
+    nxt(pv, "sdf")
+
+    aff(A("opa"), A("pai"))
+    aff(A("osd"), A("sdi"))
+    aff(A("btf"), A("bti"))
+    aff(A("th0"), A("btf"), 1e6)
+    aff(A("th1"), A("btf"), -1e6, 1e6)
+    aff(A("ro0"), A("btf"), 2.0)
+    aff(A("ro1"), A("btf"), -2.0, 2.0)
+    for t in range(2):
+        ts(A("th%d" % t, 0, 1), A("th%d" % t, 0, 1), cb, None, ALU.max)
+        ts(A("ro%d" % t, 0, 1), A("ro%d" % t, 0, 1), cnz, None, ALU.mult)
+    ts(A("xj"), A("iti"), 896, None, ALU.bitwise_and)
+    ts(A("xk"), A("iti"), 3, 15, ALU.logical_shift_right, ALU.bitwise_and)
+    ts(A("x3"), A("iti"), 7, None, ALU.bitwise_and)
+    aff(A("t1"), A("x3"), 16.0)
+    tt(A("t2"), A("xj"), A("xk"), ALU.add)
+    tt(A("itf"), A("t1"), A("t2"), ALU.add)
+    ts(A("itf", 0, 1), A("itf", 0, 1), cnz, cz, ALU.mult, ALU.add)
+    digits("ith", "itl", "itf")
+    aff(A("oit"), A("itf"))
+    torow("att", IT, 0, "ith")
+    torow("att", IT + 1, 0, "itl")
+    for q in range(16):
+        aff(A("us", q, W, 16), A("un", M * q, M * (q + 1)))
+
+    others = [r for r in range(N) if r != rank]
+    eng = topo.engines(core, T.cores[others[0]])
+
+    def dst(r):
+        a = topo.addr(T.cores[r])
+        return DstId(rid=a[0], pnc=a[1])
+
+    def walk(t):
+        nb[1] = 6
+        acc = [A("ps6"), A("ps7")]
+        S = lambda n, s: A(n, MI * s, MI * (s + 1))
+        for s in range(4):
+            gw = "gw%d" % (s % 2)
+            if s == 0:
+                g2(gw, A("ge"), "ow")
+                tt(A("hx"), fold(sig("vv", gw, 0)), A("h3"), ALU.min)
+                pn, prev = A("hx"), A("hs")
+            else:
+                g2(gw, A("tab", 0, 2 * W), "ow", MI * s)
+                pn, prev = fold(sig("nx", gw, 0)), S("sck", s - 1)
+            if s < 3:
+                if TTU:
+                    tt(S("ow", s + 1), pn, prev, ALU.max)
+                    tt(S("wf", s), pn, prev, ALU.max)
+                else:
+                    tt(S("wf", s), pn, prev, ALU.max)
+                    aff(S("ow", s + 1), S("wf", s))
+            ts(S("nf3", s), pn, 3072.0, 3072.0, ALU.is_ge, ALU.mult)
+            if s == 0:
+                tt(S("sck", 0), A("hs"), S("nf3", 0), ALU.min)
+            elif s == 1:
+                tt(S("sc", 1), fold(sig("sd", gw, 0)), S("sck", 0), ALU.add)
+                tt(S("sck", 1), S("sc", 1), S("nf3", 1), ALU.min)
+            ttu(S("om", s), S("wm", s), A("hdf") if s == 0 else S("wn", s - 1), S("nf3", s), ALU.min)
+            if s < 3:
+                tt(S("wn", s), S("wf", s), S("nf3", s), ALU.subtract)
+            for h in range(2):
+                gather("gu%d" % s, A("un", 0, W), ("om", MI * s), 32 * h, 32 * h + 32)
+                mm(acc[h], [(A("idn"), A("gu%d" % s, 512 * h, 512 * h + 512))], s == 0, s == 3)
+        snd, lnd, kt = "snd%d" % t, "lnd%d" % t, "kt%d" % t
+        for h in range(2):
+            aff(A(snd, 512 * h, 512 * h + 512), acc[h])
+        nb[1] = 8
+        tr = [RemoteDMATransfer(dst_ids=[dst(r)], dma_engine_mask=1 << eng[i], remote_sem=T.sem["rs%d" % t],
+                                src=T[snd][:, 128 * r:128 * (r + 1)], dst=T[lnd][:, 128 * rank:128 * (rank + 1)])
+              for i, r in enumerate(others)]
+        k1 = op("g", 0.5, lambda e: g.remote_dma_fused(tr, local_sem=T.sem.loc), [A(snd)], [], lat=REML, kind=("rs%d" % t, N - 1, N - 1))
+        pt_ = bank(128)
+        mm(pt_, [(A("idn"), A(snd if r == rank else lnd, 128 * r, 128 * (r + 1))) for r in range(N)], ext=[k1])
+        ts(A("gev"), pt_, cth, 0.5, ALU.is_ge, ALU.subtract)
+        pc = fold([(A("bo"), A("gev"))], 128)
+        own = A(kt, 128 * rank, 128 * (rank + 1))
+        ts(own, pc, 0.5, 0.5, ALU.is_ge, ALU.subtract)
+        mask = 0
+        for e_ in eng:
+            mask |= 1 << e_
+        tr2 = [RemoteDMATransfer(dst_ids=[dst(r) for r in others], dma_engine_mask=mask, remote_sem=T.sem["kv%d" % t],
+                                 srcs=[own[0]], dsts=[own[0] for r in others])]
+        k2 = op("g", 0.5, lambda e: g.remote_dma_fused(tr2, local_sem=T.sem.loc), [own], [], lat=REML,
+                kind=("kv%d" % t, (N - 1) * len(eng), len(eng)))
+        aff(A("t7", 0, 128), pt_)
+        for m in range(8):
+            aff(A("yas", 128 * t + m, 128 * (t + 1), 8), A("t7", 16 * m, 16 * m + 16))
+        return k2
+
+    def pre_par():
+        g6("ga", A("att"), "opa")
+        aff(A("oip"), whole("it", "ga"))
+        aff(A("p2f"), whole("pa", "ga"))
+
+    def pre_side():
+        b = fold([(wq("sd", q), A("att", q, W, 16)) for q in range(16)], M)
+        ts(A("t3"), b, 0.0, 8192.0, ALU.is_equal, ALU.mult)
+        tt(A("t4"), A("t3"), A("sf3"), ALU.min)
+        ttu(A("osc"), A("t3"), b, A("t4"), ALU.max)
+        win = A("pt")
+        for c in range(12):
+            src, f = A("att", 256 * c, 256 * c + 256), A("osc", 16 * c, 16 * c + 16)
+            op("v", FIX + CY * SC * 256, lambda e, src=src, f=f: g.vector.tensor_copy(win[0].indirect(f[0]), src[0]), [src, f], [win])
+        g6("gb", A("att"), "osd")
+        aff(A("sgs"), whole("sg", "gb"))
+        tt(A("d2"), whole("sd", "gb"), A("sdf"), ALU.subtract)
+        b = fold(nat("sg", "pt"), M)
+        tt(A("t5"), b, A("sgs"), ALU.subtract)
+        tt(A("t6"), A("t5"), A("btf"), ALU.mult)
+        ttu(A("op1"), A("t5"), b, A("t6"), ALU.subtract)
+        ttu(A("op0"), A("t4"), A("sgs"), A("t6"), ALU.add)
+        ts(A("dq"), fold(nat("rq", "pt"), M), cq, None, ALU.subtract)
+        tt(A("dm"), fold(nat("rm", "pt"), M), A("mf"), ALU.subtract)
+
+    def post(t, kv):
+        kt = A("kt%d" % t)
+        g6("gc2", kt, "oip", ext=[kv])
+        b = bank(M)
+        for j in range(3):
+            mm(CH(b[1], j), sig("kp", "gc2", j) + [(A("idn"), CH("pah", j)), (A("idn"), CH("pal", j))])
+        tt(A("tj"), b, A("p2f"), ALU.max)
+        ts(A("opm"), b, 4096.0, 3072.0, ALU.add, ALU.min)
+        g6("gf", kt, "oit", ext=[kv])
+        for j in range(3):
+            b = fold(sig("kn", "gf", j) + [(A("idn"), CH("nh", j)), (A("idn"), CH("nl", j))])
+            tt(CH("xj", j), b, CH("tj", j), ALU.max)
+            tt(CH("eb", j), b, CH("th%d" % t, j), ALU.is_ge)
+            ts(CH("xk", j), CH("xj", j), 4095, None, ALU.bitwise_and)
+            digits("jh", "jl", "xk", 64 * j, 64 * j + 64)
+        for c0 in (0, W, 2 * W):
+            torow("tab", JJ, c0, "jh")
+            torow("tab", JJ + 1, c0, "jl")
+        g6("ua", A("un"), "opm", add="us")
+        g6("gc2", A("tab", 0, W), "opa")
+        for j in range(3):
+            aff(CH("od", j), fold(sig("jj", "gc2", j) + [(A("id3"), CH("eb", j)), (A("id3"), CH("ro%d" % t, j))]))
+        g6("gd", A("tab"), "od")
+        aff(A("oi"), whole("jj", "gd"))
+        g6("gf", A("gd"), "op%d" % t)
+        for j in range(3):
+            b = bank()
+            mm(b, sig("md", "gd", j), True, False)
+            mm(b, sig("mf", "gf", j), False, True)
+            ts(CH("mb", j), b, 28672.0, None, ALU.is_equal)
+            ts(CH("ma", j), b, 20480.0, None, ALU.is_equal)
+            tt(CH("deh", j), CH("mb", j), CH("dq", j), ALU.mult)
+            tt(CH("del", j), CH("mb", j), CH("dm", j), ALU.mult)
+            ttu(CH("osm", j), CH("t1", j), CH("ma", j), CH("sgs", j), ALU.mult)
+        torow("tab", DL, 0, "deh")
+        torow("tab", DL + 1, 0, "del")
+        if t == 0:
+            tt(A("t2"), A("ma"), A("d2"), ALU.mult)
+            aff(A("t3"), A("mb"), 1e6)
+            tt(A("t4"), A("t2"), A("sdf"), ALU.add)
+            tt(A("t5"), A("t4"), A("t3"), ALU.subtract)
+            relu(A("sd1"), A("t5"))
+            digits("sdh", "sdl", "sd1")
+            tt(A("th1"), A("t3"), A("th1"), ALU.max)
+            torow("att", SD, 0, "sdh")
+            torow("att", SD + 1, 0, "sdl")
+            g2("gu1", A("att"), "ow")
+            aff(A("hs"), fold(sig("sd", "gu1", 0)))
+        g6("ub", A("ua"), "osm")
+        for q in range(1, 16, 2):
+            b = bank(2 * M)
+            for h in range(2):
+                mm(A(b[1], M * h, M * h + M), [(A("idn"), A(x, q - 1 + h, W, 16)) for x in ("ua", "ub")])
+            ts(A("un", M * (q - 1), M * (q + 1)), b, 15.0, None, ALU.min)
+            if q % 4 == 3:
+                a = A("un", M * (q - 3), M * (q + 1))
+                if t == 0:
+                    ge4(A("ge", a[2], a[3]), a)
+                else:
+                    dma(T.yc[:, a[2]:a[3]], a[0], [a], [], lat=3.0)
+        g6("gc2", A("tab", 0, W), "oi")
+        if t == 0:
+            torow("tab", SD, 0, "sdh")
+            torow("tab", SD + 1, 0, "sdl")
+            g2("gu2", A("gc2"), "osh")
+            aff(A("h3"), fold(sig("rp", "gu2", 0)), 1.0, 3072.0)
+            b = whole("rp", "gc2")
+            aff(A("pa3"), b, 1.0, 3072.0)
+            aff(A("paf"), b)
+            pv = bank(M)
+            for j in range(4):
+                mm(pv, nat("vv", "ge", range(4 * j, 4 * j + 4)), j == 0, j == 3)
+            nxt(pv, "sd1")
+            aff(A("opa"), A("paf"))
+            digits("pah", "pal", "paf")
+            torow("att", PA, 0, "pah")
+            torow("att", PA + 1, 0, "pal")
+        else:
+            aff(A("ypf"), whole("rp", "gc2"))
+            dma(T.yp[:], T.ypf[:], [A("ypf")], [])
+
+    kv = walk(0)
+    torow("tab", ID, 0, "idq")
+    torow("tab", ID + 1, 0, "idm")
+    torow("tab", FL, W, "one")
+    torow("tab", FL, 2 * W, "twos")
+    pre_par()
+    pre_side()
+    post(0, kv)
+    kv = walk(1)
+    dma(T.ya[:], T.yas[:], [A("yas")], [])
+    for q in range(16):
+        aff(A("us", q, W, 16), A("un", M * q, M * (q + 1)))
+    pre_par()
+    post(1, kv)
+    return ops
+
+
+def plan(ops):
+    if ORDER.strip():
+        order = [(int(w[:-1], 16), w[-1], 0.0) for w in ORDER.split()]
+        assert sorted(k for k, _, _ in order) == list(range(len(ops)))
+        return order, 0.0
+    return [(k, o["engs"][k % len(o["engs"])], 0.0) for k, o in enumerate(ops)], 0.0
+
+
+def rank_program(g, core, T, topo):
+    rank = T.rank_of(core)
+    if rank is None:
+        return
+    ops = build(g, T, topo, core, rank)
+    order, _ = plan(ops)
+    queue = {"v": g.vector, "a": g.scalar, "p": g.tensor, "s": g.sync, "g": g}
+    count = {"cv": 0, "ca": 0, "cp": 0, "cg": 0, "loc": 0}
+    done, where = {}, {}
+    seen = {e: {} for e in queue}
+    nd = 0
+    for k, e, _ in order:
+        o = ops[k]
+        assert e in o["engs"]
+        need = {}
+        for j, hard in o["deps"].items():
+            if where[j] == e and ops[j]["kind"] == "c" and o["kind"] == "c" and (e == "p" or not hard):
+                continue
+            s, v = done[j]
+            need[s] = max(need.get(s, 0), v)
+        for s, v in need.items():
+            if seen[e].get(s, 0) < v:
+                queue[e].wait_ge(T.sem[s], v)
+                seen[e][s] = v
+        ins = o["fn"](e)
+        where[k] = e
+        if o["kind"] == "c":
+            s = "c" + e
+            count[s] += 1
+            ins.then_inc(T.sem[s], 1)
+            done[k] = (s, count[s])
+        elif o["kind"] == "d":
+            s = "d%d" % nd
+            nd += 1
+            ins.then_inc(T.sem[s], 16)
+            count[s] = 16
+            done[k] = (s, 16)
+        else:
+            s, v, loc = o["kind"]
+            count[s] = v
+            count["loc"] += loc
+            done[k] = (s, v)
+    for s, v in count.items():
+        if v > 0 and max(seen[e].get(s, 0) for e in seen) < v:
+            g.wait_ge(T.sem[s], v)

@@ -3,11 +3,14 @@ from concourse.mybir import AluOpType as ALU, ActivationFunctionType as AF
 
 W, M, I, MI = 3072, 192, 1024, 64
 BF, F, I32, U16 = "bfloat16", "float32", "int32", "uint16"
-NX, SD, JJ, FL, ID, DL, PA, IT = 0, 2, 4, 6, 7, 9, 11, 13
-WV = {"vv": None, "pa": {11: 1, 12: 1}, "sd": {2: 1, 3: 1}, "nx": {0: 1, 1: 1}, "sg": {7: 1, 8: 16},
-      "jj": {4: 1, 5: 1}, "mf": {4: 1, 5: 1, 6: 4096}, "md": {4: -1, 5: -1, 6: 12288},
-      "rp": {7: 192, 8: 1, 9: 192, 10: 1}, "rq": {7: 1}, "rm": {8: 1},
-      "it": {13: 1, 14: 1}, "kp": {0: 8192}, "kn": {0: 16384}}
+RA, RE, RC, RB, IT, R1, R0, SD, NX = 0, 2, 4, 6, 8, 10, 11, 12, 14
+KEPT, DROP, BIG = I, I + 8, 8192.0
+WV = {"vv": None, "id": {0: 1, 1: 1}, "nx": {14: 1, 15: 1}, "sd": {12: 1, 13: 1}, "pa": {6: 1, 7: 1},
+      "nsd": {12: -8192, 13: -8192}, "it": {8: 1, 9: 1}, "bit": {10: 1}, "itb0": {8: 1, 9: 1, 10: BIG}, "itb1": {8: 1, 9: 1, 10: -BIG},
+      "r1n": {10: -BIG}, "r0n": {11: -BIG}, "itr0": {8: 1, 9: 1, 11: -BIG}, "itr1": {8: 1, 9: 1, 10: -BIG},
+      "a0": {0: 1}, "a1": {1: 1}, "nxd": {2: 1, 3: 1, 4: 1, 5: 1, 14: 4096}, "nxs": {2: 1, 3: 1, 4: 1, 5: 1},
+      "val": {0: 1, 1: 1, 6: 1, 7: 1}, "nval": {0: -1, 1: -1, 6: -1, 7: -1}, "kd": {4: W},
+      "rp": {0: 1, 1: 1, 2: 1, 3: 1}, "h": {11: DROP}, "sg": {0: 1 / 192, 1: 16}}
 WOFF = {k: 144 * i for i, k in enumerate(WV)}
 
 SCRATCH = {}
@@ -18,60 +21,70 @@ def _sb(names, cols, dty):
         SCRATCH[n] = ("sbuf", [128, cols], dty)
 
 
-_sb("tab", 3 * W, BF)
-_sb("pt", 2 * W, BF)
-_sb("att us ua ub ge ga gb gc2 gd gf", W, BF)
-_sb("un", W + 16, BF)
+_sb("tab pt", 2 * W, BF)
+_sb("un uc ua ub sm ge ga gb a1 k0 l2 g5 g6 g7", W, BF)
+_sb("l3", W + 16, BF)
 _sb("wv", 144 * len(WV), BF)
-_sb("idn id3 bo ones gev", 128, BF)
+_sb("idn nid bo f128 ones gev", 128, BF)
+_sb("zz", 512, BF)
 _sb("kt0 kt1", I + 16, BF)
 _sb("snd0 snd1 lnd0 lnd1 gw0 gw1 gu0 gu1 gu2 gu3", I, BF)
 _sb("yas", 256, F)
-_sb("pai sdi iti bti x3 xj xk", M, I32)
-_sb("hdi", MI, I32)
-_sb("thi pi", 4, I32)
-_sb("col", 8, F)
-_sb("mf nf sf3 paf pa3 sdf sd1 btf itf p2f t1 t2 t3 t4 t5 t6 t7 xx nx0 th0 th1 sgs d2 ma mb tj ypf", M, F)
-_sb("pah pal sdh sdl ith itl idq idm nh nl one twos ro0 ro1 eb jh jl dq dm deh del n0h n0l n1h n1l", M, BF)
-_sb("opa osd oit oip opm od oi op0 op1 osm osc", M, U16)
+_sb("ints", 4 * M + MI, I32)
+_sb("hi lo", 3 * M + MI, BF)
+_sb("pi", 4, I32)
+_sb("thi", 4, I32)
+_sb("col", 12, F)
+_sb("mf pa3 sdf sd1 sdt sa0 sa1 o1f t1 t3 ds ypf nbf op0 op1 p1f", M, F)
+_sb("idq idm idq3 r0 r1 pen0 pen1 pb0 pb1 n0h n0l n1h n1l dq0 dm0 dq1 dm1 hit deh del sdh sdl pah pal one", M, BF)
+_sb("opa osd osc oip opm o2 o3 oi opk oit0 oit1 ox osm", M, U16)
 _sb("ow om", 4 * MI, U16)
+_sb("hdf h3 hs", MI, F)
 _sb("osh", MI, U16)
-_sb("hdf h3 hs hx", MI, F)
-_sb("wf nf3 sck sc wn wm", 4 * MI, F)
+_sb("wf sck sc wn", 4 * MI, F)
 for _b in range(8):
     SCRATCH["ps%d" % _b] = ("psum", [128, 512], F)
 
-NDMA = 72
-SEMAPHORES = ["cv", "ca", "cp", "cg", "rs0", "rs1", "kv0", "kv1", "loc"] + ["d%d" % i for i in range(NDMA)]
-
-CY, PCY, GA, SC, FIX, HOP = 1.04e-3, 0.5e-3, 1.56, 3.8, 0.06, 0.15
-DMAL, REML = 2.3, 5.5
-TTU = True
+NDMA = 76
+SEMAPHORES = ["cv", "ca", "cp", "cg", "loc"] + [s + x for s in ("rs", "kv") for x in ("00", "01", "10", "11")] + ["d%d" % i for i in range(NDMA)]
+PAI, SDI, HDI, ITI, BTI = 0, M, 2 * M, 2 * M + MI, 3 * M + MI
+NCH = 6
+NH = 2
+SCH = 256
+G6A = (2, 3)
+PRE = (0, 1)
 ORDER = """
-9a es 11v 37g ca fs 0a 2s 1a 3s ba 10s 5s 7a 4s aa 8a 6a da 44v 13g 14g 1ag 4fa 4bv 18g 4av 1bg 12v 3cv 5ds 19g 52v 36g 97a 53v 54a 15v 3dv 5ea 55v 58s 56a 94a 6dv 5as 59s 9aa 99a 47v 6bv 3fa 16g 3ea 49v 6fa 17g 61v 1eg 57v 6cp 3ag 4ev 71a 5bs 6ep 62v a3v 5cs 45v 70p 9da 9ca 72p 9fa 30g 95a 32g a2a 39g 73v 96a 5fs 60s 40v 98a 74v 42a 63a 46v 64a 38g 7fv a1a 65p 8av 77a 35v 75a 89v 7bs 67p a4a 8bv 79s 43v 1cg 76v 1fg 33g a5a 4cv 69p 7as 78v 3bg 88v 82a 7cs a6p 6av 68a 8cv 9ea 41a 48v 66a 83a 8dv 81a 2eg a7v 80a eas 8ev 2dg a9v 2cg 8fa aav 1dg a8v a0a acv 25g 92s 50a 90v 20g 2fg b3a 21g b2v 28g 93s 29g 9ba 2ag 87v b0a 85v b4p adv 2bg abv 31g 84v 22g b5v 7dv 23g b1p c1a b6v 26g c2v b8p 24g 27g 34g aea b7v b9v c3p bbv bav bfa bcv afp 86v 91v f9p 4dv c4v bda cdv cea c5v c0p c6v bep c7v eba fav cfp e9s e7s c8v e8s fbv cba d0v fcv d1v c9v d4a ccp fdv cap d2a d5p d7a d3p fev d6a eda d8g ffv efa 100v eca 101v eea f1p f5p f0a 7ev 102v f6p 109a f7p 103v 10ea f2p 10aa 51v d9p f8v dav 10ca dbp dev f3p dcv 104v ddg 10da 113p 10fp e5v dfa e2a 105v e0a e3a e4a 10ba e1v 106v e6a 114p 115p f4v 107v 110p 111p 108v 112a 117p 120a 124v 121v 12ba 122v 123a 126p 125v 12da 127p 116v 12ea 128p 12cv 130a 137p 118v 129v 131p 12fa 138v 13av 12av 132v 13bv 134v 13dp 13cv 135v 133v 136v 11cp 13ev 139v 140v 13fv 141v 142v 145s 143s 119v 147s 144s 146s 148s 11ep 11dv 14av 149v 152a 14cv 14fa 150v 151a 11av 155p 14bv 153a 157p 156v 14dv 154a 11fv 15ba 14ev 159p 15ca 158v 15av 15dv 15ea 16bp 15fv 161p 160a 172p 11bv 179p 165a 166v 169a 16av 16cp 167a 16dv 17ap 16ev 171v 162p 17bv 168a 17cv 17dv 17fv 191v 190a 173p 163p 17ev 194a 170v 174v 16fv 175v 176v 195a 178v 180s 177v 182v 181s 183v 193a 184v 185v 192a 164v 186v 189v 196p 187a 1b2a 197p 188v 18as 1a7p 199p 1b4v 18bs 19dp 1b6a 19ap 19ep 198v 1a4p 1b3a 1abp 19fv 1a5p 1a0p 19bv 1a8p 21ba 1acp 21ev 21aa 1bep 21cv 1a9v 18ca 1a1p 18dv 1b5a 1a6v 18ep 1a2v 1b7a 1bfp 18fv 19cv 1aep 1adv 1b8s 1bba 1afp 1b9s 1c3p 1a3v 1c0p 1b0v 1baa 1aav 1c4p 227v 225a 1c5p 1b1v 1c1a 224v 1c2a 1c6p 226v 228v 1d6a 1d1v 1bcp 1c7v 1c8v 1cba 1d2a 1ccv 1cfs 1c9a 1d4s 1d7a 1bdv 1cds 1cav 1d0s 223v 1ces 1d3v 229a 1d8p 222a 21dv 221a 1d5s 220v 21fa 1d9v 1dcv 1dev 1dav 1e0a 1dbv 1dfv 1ddv 1e4v 1e5a 1e1p 22bv 22fa 1e6p 1eap 1e7v 1e8v 1f4a 1f3v 1e2a 1e9v 1ebv 1f5p 1edv 1ecv 1eev 1efa 1f6v 1e3p 1f7v 1f8v 200v 1ffa 1f0p 1f9v 1f1a 1fav 201p 1fdv 1fba 1f2p 202v 203v 1fep 204a 206v 1fcp 22ea 207p 205p 209v 208a 22av 22da 20ag 234p 22ca 230p 235p 231p 236p 232p 237v 233v 20bp 20cv 20dp 210a 20ev 216a 215v 217a 218v 211a 20fg 212a 213a 214a 219s 238a 23dv 239a 23av 23bv 23ca 23ep 243a 244v 23fp 245v 246a 240p 249p 241v 248a 247v 24fp 24av 250v 255p 24bv 24cv 242v 24dv 256v 252v 258v 257v 259v 253v 25av 25ds 254v 25bs 25fs 24ev 261v 25cs 260s 25es 262v 251v 267a 268v 26bv 26ca 26dp 26aa 26ev 271p 269v 274a 272v 266v 26fp 278a 270v 273v 276a 275v 279p 277a 283p 264v 27ap 27ea 28ap 263v 27da 27bp 265v 291p 281a 284p 280v 27fa 285v 27cv 282a 286v 28bp 289v 287v 288v 29aa 28cv 292p 28fv 28dv 28ev 293v 29ba 294v 295v 296v 298s 290v 299s 297v 29ea 29fv 29cv 29da 2a7p 2bca 2bfv 2b8p 2a8p 2a0p 2aap 2a9v 2bda 2a3p 2b9p 2a1p 2bav 2aep 2c1a 2b1p 2a2v 2b5p 2a4p 2abp 2bea 2a5v 2b2p 2c2p 2acv 2a6s 2c0a 2b6p 2b3v 2ads 2afp 2b7v 2c3p 2b0v 2bbs 2c4p 2b4s 2c5v 2c6s
+1s 2s av cg 0a 64v 6s dg 3a ev 8a 1cv fa 65v 15a 18a 27v 17v 79v 68v 66v 77a 5s 1bv 19g 7av 7bv 7s 1ag 16a 9s 81a 4s 80s 84s 86s a1a 20v 2ag 2bg 83a 89v 82s 88v 7es 7fs 28g 7ds 29g 2cg 1da 69a a2p a3v a4p 95v 14a 1fg 87s 9av 9bv 96v 1eg 97v a5a 2dg 2eg 9ev 30g 8ap 67v a7a 85s 25g a6p bv 7cs 34g 8bv 8dv 31g a8p a9v 9ca 9dv aav adv 8ea 99s a0s 8fp 98s 2fg 91p 6ev 60g b1s 5eg 5fg c3a 11g 32g 33g aba afs 23g aev acv b2s c2a c4p 63v 143p 13cp 8ca 10v 36g 92v 37g 61g 22v 21v 9fs 78v b0s 90a c5v c6v 12a 46g c7v 26g b4s 24a 13a 58g 3dg 6av 47g 93p 54g b9p bap 55g c8v c9v cav 6dv d0a 50g d1v 4cg 4dg 73a 38g ccv 75a 62g cea 74a d2p bbp 6fv 3ag d3v dfa d4v 39g 56g 35g 48g 6ba b3s 76a e0v 6ca bcv bda 42g 3fg d6p d5v d7v cbv d8v d9v dav 4eg e1p e2v 49g 51g bep 59g 40g 4ag bfp c0p 45g 52g e3v 57g 41g 3bg 71v 121a e4v 5dg ebv 43g 5ag e5v e6v cfp 44g 5bg dba cdp dcp eca edp e7v c1v 127p b5p b6p b7p 70v 53g 123a dda 115v dep e9a eap eev 94v efv f2a 4bg 116v 3cg f0a f3p 72v f5a 117v e8p f1p f4a b8v 118v 119v 11av 128p 129p 4fg 11bv 11cv ffg 100w 122a 14ap 14bp 125a 12aa 130p f6g f7w 5cg 124a 131p 126a 109a 10ba 101p 102v 107a 10ca 11dv 132p 103p 104v 105g 106w 108a 14cp 14dp 11ev 10aa f8p f9v fap fbv fcg 11fv 120v 10da 10ep 10fp 110p 112s 12ba 12fv 3eg 14ev 14fv 111v 133v 12ca 12da 134p 12ev 135p 136p 137v fdw 114a 113s 154v 138p 139p 144p 145p 155v 159a 156a 15ba 151v 157a 153v 13dp 150v 13ep fea 164p 165v 13fp 140p 13ap 158a 152v 166v 167v 15aa 15cp 15dv 15ev 13bv 170a 160p 161v 247p 162v 176v 171a 180p 17as 177v 17bs 243p 168p 169p 16ap 141v 163v 174v 16ca 16fa 175v 15fv 178s 181v 16da 16ea 186a 248p 179s 173v 17ep 17fv 184v 244p 17cp 146p 147p 187a 17dv 183v 185a 189p 148v 16bv 182a 18bp 18cp 18dp 194v 193a 192v 191a 195a 172v 196a 1a4p 1a5v 1a6v 1a7v 1bbv 18ep 18fa 190v 197p 198p 199p 19ap 19bv 19cv 19dv 19fa 1acv 19es 1ada 188p 1a0p 1a1v 18ap 1afv 1a2v 1a3v 1bav 1b0a 1b2s 1b7a 1a8p 1a9v 1aav 1b1v 1bdv 1bcv 1b4a 1b8p 1b9a 1abv 1b5p 1b6a 1bev 245p 1c2v 1b3s 1aes 1cav 1cev 249p 1ccv 1bfp 1c0a 1c1p 1c3p 1cfv 1c4a 1c5p 1cba 1cda 1c7a 1d0p 1d1v 1d4p 1d5v 1f5a 1dcv 1e0v 1d6a 1d2a 1d3v 1d8p 1c6a 1e1v 1e4v 1d7v 1e5v 1d9a 1dav 1e6v 1f0s 1e2a 1dbv 1e7v 1eav 1f1s 1ees 1dda 1e8a 1e3v 1f4a 1ecs 1ebv 1e9v 1c8p 24av 24bv 1efs 1eds 142v 1dep 149v 1dfa 1c9a 1f6p 1f7v 1f8v 203a 23bp 23cp 1f9v 1fav 1fbv 1fcv 202v 1fea 1f2s 200v 204p 205v 206v 1fdv 212a 211v 208p 209v 207v 262a 20av 20bv 20cv 23dp 20da 213p 214v 215v 21ev 216v 217v 218v 219v 23fp 21da 21fp 1f3s 1ffp 21ba 20fa 201p 20ep 220v 221v 21ap 224a 222v 223p 226a 210p 21cp 225p 23ev 25ev 227a 240p 241p 25fv 260v 265p 24ea 24da 24cv 252p 242v 246v 261a 250a 24fv 228g 229w 22ap 22bv 22cp 230a 251a 231g 264a 232w 233p 22dv 22eg 22fw 25dv 234v 263a 235p 236v 239a 23as 253p 254p 256a 258a 259v 25bv 266p 267p 255v 268v 25cv 237g 238w 272a 273a 26fa 270a 25av 257s 269v 285p 26cv 28bp 26ev 28fp 26bv 26dv 277p 26av 278v 290v 293s 27bp 279p 27av 275p 276v 280v 27fv 274a 271a 281a 28dp 27cp 27dp 282a 283a 296p 28cv 297v 284a 29da 28ev 294p 295v 29cv 29aa 298p 299v 29fa 289p 29ea 29bv 27ev 2a9a 287p 292s 2a0p 28av 2a3p 2a4p 2a5p 2a6p 286v 2aba 2aav 2aev 2adv 2b8p 2b9v 2bav 2afp 288v 2aca 2b0p 2a7a 2b1p 2b2p 2b3v 2b4v 2b5v 2c5a 291s 2b6s 2a8v 2a1p 2bbp 2bcv 2bdv 2cdv 2a2p 2bep 2bfv 2c0v 2cev 2b7a 2c9a 2d0v 2d3v 2d6v 2c1a 2c2p 2d9a 2dba 2cap 2daa 2c6p 2e0p 2d8a 2dep 2d4v 2d5s 2d7a 2d1v 2d2s 2cfs 2c3v 2c4s 2cbv 2ccs 2e1a 2c7v 2c8s 2dfa 2dcp 2ddv 2e2s
 """
 
 
-def build(g, T, topo, core, rank):
+def build(g, T, topo, core, rank, place=None):
     ops = []
     log = {}
     N = len(T.cores)
+    where = {}
 
     def A(name, c0=0, c1=None, step=1, row=None):
+        buf = name
+        if name.startswith("ps"):
+            buf = "ps%d" % (place[name] if place else 0)
         if c1 is None:
-            c1 = SCRATCH[name][1][1]
+            c1 = SCRATCH[buf][1][1]
         if row is not None:
-            ap = T[name][row::16, c0:c1]
+            ap = T[buf][row::16, c0:c1]
         elif step != 1:
-            ap = T[name][:, c0:c1:step]
+            ap = T[buf][:, c0:c1:step]
         else:
-            ap = T[name][:, c0:c1]
+            ap = T[buf][:, c0:c1]
         return (ap, name, c0, c1, row, len(range(c0, c1, step)), step)
 
-    def two(*a):
-        return all(SCRATCH[x[1]][2] in (BF, U16) for x in a)
+    def dty(x):
+        return F if x[1].startswith("ps") else SCRATCH[x[1]][2]
 
-    def op(engs, dur, fn, R, Wr, lat=0.0, kind="c", ext=()):
+    def two(*a):
+        return all(dty(x) in (BF, U16) for x in a)
+
+    def op(engs, dur, fn, R, Wr, lat=None, kind="c", ext=()):
         k = len(ops)
         deps = {}
         for acc, wr in ((R, False), (Wr, True)):
@@ -97,250 +110,264 @@ def build(g, T, topo, core, rank):
             deps[j] = True
         if not isinstance(dur, dict):
             dur = {e: dur for e in engs}
-        ops.append({"engs": engs, "dur": dur, "fn": fn, "deps": deps, "lat": lat, "kind": kind, "tag": (Wr or R)[0][1]})
+
+        def run(e, k=k):
+            where[k] = e
+            return fn(e)
+        ops.append({"engs": engs, "dur": dur, "fn": run, "deps": deps, "lat": lat, "kind": kind, "tag": (Wr or R)[0][1],
+                    "banks": sorted(set(a[1] for a in list(R) + list(Wr) if a[1].startswith("ps")))})
         return k
 
     def sc_ap(s):
         return s[0] if isinstance(s, tuple) else s
 
+    def cyc(n, half=False):
+        return ("c", max(64, n * (0.5 if half else 1)))
+
     def ts(out, in0, s1, s2, op0, op1=None):
         rd = [in0] + [s for s in (s1, s2) if isinstance(s, tuple)]
-        d = FIX + CY * max(64, out[5] * (0.5 if two(out, in0) else 1))
         if op1 is None:
             fn = lambda e: g.vector.tensor_scalar(out[0], in0[0], sc_ap(s1), None, op0)
         else:
             fn = lambda e: g.vector.tensor_scalar(out[0], in0[0], sc_ap(s1), sc_ap(s2), op0, op1)
-        return op("v", d, fn, rd, [out])
+        return op("v", cyc(out[5], two(out, in0)), fn, rd, [out])
 
     def tt(out, a, b, alu):
         ps = a[1].startswith("ps") or b[1].startswith("ps")
-        d = FIX + CY * max(64, out[5] * (1 if ps else 2))
-        return op("v", d, lambda e: g.vector.tensor_tensor(out[0], a[0], b[0], alu), [a, b], [out])
-
-    def ttu(out, tmp, a, b, alu):
-        if TTU:
-            return tt(out, a, b, alu)
-        tt(tmp, a, b, alu)
-        return aff(out, tmp)
+        return op("v", cyc(out[5] * (1 if ps else 2)), lambda e: g.vector.tensor_tensor(out[0], a[0], b[0], alu), [a, b], [out])
 
     def aff(out, in0, mul=1.0, add=0.0):
-        fl = all(SCRATCH[x[1]][2] in (BF, F) for x in (out, in0))
+        fl = all(dty(x) in (BF, F) for x in (out, in0))
         plain = mul == 1.0 and add == 0.0
+        ad = add[0] if isinstance(add, tuple) else float(add)
 
         def fn(e):
             if e == "a":
                 if plain:
                     return g.scalar.activation(out[0], in0[0], AF.Copy)
-                return g.scalar.activation(out[0], in0[0], AF.Identity, bias=float(add), scale=float(mul))
+                return g.scalar.activation(out[0], in0[0], AF.Identity, bias=ad, scale=float(mul))
             if plain:
                 return g.vector.tensor_copy(out[0], in0[0])
-            return g.vector.tensor_scalar(out[0], in0[0], float(mul), float(add), ALU.mult, ALU.add)
-        d = {"v": FIX + CY * max(64, out[5] * (0.5 if two(out, in0) else 1)), "a": FIX + CY * max(64, out[5])}
-        return op("va" if fl else "v", d, fn, [in0], [out])
-
-    def relu(out, in0):
-        def fn(e):
-            if e == "a":
-                return g.scalar.activation(out[0], in0[0], AF.Relu)
-            return g.vector.tensor_scalar(out[0], in0[0], 0.0, None, ALU.max)
-        return op("va", FIX + CY * max(64, out[5]), fn, [in0], [out])
+            return g.vector.tensor_scalar(out[0], in0[0], float(mul), ad, ALU.mult, ALU.add)
+        d = {"v": cyc(out[5], two(out, in0)), "a": cyc(out[5])}
+        return op("va" if fl else "v", d, fn, [in0] + ([add] if isinstance(add, tuple) else []), [out])
 
     def ge4(out, in0):
         def fn(e):
             if e == "a":
                 return g.scalar.activation(out[0], in0[0], AF.Sign, bias=-3.5)
             return g.vector.tensor_scalar(out[0], in0[0], 4.0, 0.5, ALU.is_ge, ALU.subtract)
-        return op("va", {"v": FIX + CY * out[5] * 0.5, "a": FIX + CY * out[5]}, fn, [in0], [out])
+        return op("va", {"v": cyc(out[5], True), "a": cyc(out[5])}, fn, [in0], [out])
 
     def mset(out, val):
-        d = FIX + CY * max(64, out[5] * (0.5 if two(out) else 1))
-        return op("v", d, lambda e: g.vector.memset(out[0], val), [], [out])
+        return op("v", cyc(out[5], two(out)), lambda e: g.vector.memset(out[0], val), [], [out])
 
-    def gather(out, win, off, k0, k1, add=None, ext=()):
+    def zero(name, c0, c1):
+        for c in range(c0, c1, 512):
+            o = A(name, c, min(c + 512, c1))
+            z = A("zz", 0, o[5])
+
+            def fn(e, o=o, z=z):
+                if e == "a":
+                    return g.scalar.activation(o[0], z[0], AF.Copy)
+                if e == "g":
+                    return g.iota(o[0], [[0, o[5]]], 0, 0, allow_small_or_imprecise_dtypes=True)
+                return g.vector.memset(o[0], 0.0)
+            op("vag", {"v": cyc(o[5], True), "a": cyc(o[5]), "g": ("g", 0.13, 2 * o[5])}, fn, [z], [o])
+
+    def gather(out, win, off, k0, k1, other=None, alu=None, ext=(), clamp=False):
         o, f = A(out, 16 * k0, 16 * k1), A(off[0], off[1] + k0, off[1] + k1)
-        d = FIX + CY * GA * o[5]
-        if add is None:
+        if other is None:
             def fn(e):
                 if e == "a":
+                    if clamp:
+                        return g.scalar.activation(o[0], win[0].indirect(f[0]), AF.Relu, bias=15.0, scale=-1.0)
                     return g.scalar.activation(o[0], win[0].indirect(f[0]), AF.Copy)
+                if clamp:
+                    return g.vector.tensor_scalar(o[0], win[0].indirect(f[0]), 15.0, 15.0, ALU.min, ALU.subtract)
                 return g.vector.tensor_copy(o[0], win[0].indirect(f[0]))
-            return op("va", d, fn, [win, f], [o], ext=ext)
-        b = A(add, 16 * k0, 16 * k1)
-        return op("v", d * 1.1, lambda e: g.vector.tensor_tensor(o[0], win[0].indirect(f[0]), b[0], ALU.add), [win, f, b], [o])
+            return op("va", ("ga", o[5]), fn, [win, f], [o], ext=ext)
+        b = A(other, 16 * k0, 16 * k1)
+        return op("v", ("gt", o[5]), lambda e: g.vector.tensor_tensor(o[0], win[0].indirect(f[0]), b[0], alu), [win, f, b], [o], ext=ext)
 
-    def mm(out, terms, start=True, stop=True, ext=()):
+    def mm(out, terms, start=True, stop=True, ext=(), pick=None):
         def fn(e):
             ins = None
             for i, (l, r) in enumerate(terms):
-                ins = g.tensor.matmul(out[0], l[0], r[0], start and i == 0, stop and i == len(terms) - 1)
+                lh = l[0] if pick is None else pick()
+                ins = g.tensor.matmul(out[0], lh, r[0], start and i == 0, stop and i == len(terms) - 1)
             return ins
-        d = 0.05 + PCY * sum(max(64, r[5]) for l, r in terms)
-        return op("p", d, fn, [x for t in terms for x in t], [out], ext=ext)
+        return op("p", ("p", sum(max(64, r[5]) for l, r in terms)), fn, [x for t in terms for x in t], [out], ext=ext)
 
     def wq(v, q):
         return A("wv", WOFF[v] + 15 - q, WOFF[v] + 143 - q)
 
-    def sig(v, buf, j):
-        return [(wq(v, q), A(buf, 1024 * j + q, 1024 * (j + 1), 16)) for q in range(16)]
+    def strided(v, buf, c0, c1):
+        return [(wq(v, q), A(buf, c0 + q, c1, 16)) for q in range(16)]
 
-    def nat(v, buf, qs=range(16)):
+    def blocks(v, buf, qs=range(16)):
         return [(wq(v, q), A(buf, M * q, M * (q + 1))) for q in qs]
 
-    nb = [0, 6]
+    nb = [0]
 
     def bank(n=64):
-        b = nb[0] % nb[1]
         nb[0] += 1
-        return A("ps%d" % b, 0, n)
+        return A("ps%d" % nb[0], 0, n)
 
     def fold(terms, n=64):
         b = bank(n)
         mm(b, terms)
         return b
 
-    def whole(v, buf):
-        b = bank(M)
-        for j in range(3):
-            mm(A(b[1], 64 * j, 64 * j + 64), sig(v, buf, j))
-        return b
-
-    def dma(out, in_, R, Wr, q="s", lat=DMAL):
-        fn = lambda e: (g.sync if e == "s" else g.scalar).dma_start(out, in_)
-        return op(q, 0.1, fn, R, Wr, lat=lat, kind="d")
-
-    def torow(tabn, row, c0, src):
-        o = A(tabn, c0, c0 + W, row=row)
-        return dma(o[0], T[src][:], [A(src)], [o])
-
-    def digits(h, l, x, c0=0, c1=M):
-        aff(A(h, c0, c1), A(x, c0, c1))
-        tt(A(l, c0, c1), A(x, c0, c1), A(h, c0, c1), ALU.subtract)
-
-    def gp(dur, fn, R, Wr):
-        return op("g", dur, fn, R, Wr)
-
     def CH(name, j):
         return A(name, 64 * j, 64 * j + 64)
 
-    def g6(out, win, off, add=None, ext=()):
-        for c in range(6):
-            gather(out, win, (off, 0), 32 * c, 32 * c + 32, add, ext)
+    def thirds(v, buf, extra=()):
+        b = bank(M)
+        for j in range(3):
+            mm(CH(b[1], j), strided(v, buf, 1024 * j, 1024 * (j + 1)) + [(A(l), CH(x, j)) for l, x in extra])
+        return b
 
-    def g2(out, win, off, c0=0):
-        for h in range(2):
-            gather(out, win, (off, c0), 32 * h, 32 * h + 32)
+    def quarters(v, buf):
+        b = bank(M)
+        for j in range(4):
+            mm(b, blocks(v, buf, range(4 * j, 4 * j + 4)), j == 0, j == 3)
+        return b
 
-    for nm, src in (("pai", T.par), ("sdi", T.side)):
-        dma(T[nm][:], src[:], [], [A(nm)], q="a", lat=2.4)
+    def dma(out, in_, R, Wr, q="s", lat="row", ext=()):
+        fn = lambda e: (g.sync if e == "s" else g.scalar).dma_start(out, in_)
+        return op(q, ("d",), fn, R, Wr, lat=lat, kind="d", ext=ext)
+
+    def torow(tabn, row, c0, src, q="s"):
+        o = A(tabn, c0, c0 + 16 * src[5], row=row)
+        return dma(o[0], src[0], [src], [o], q=q)
+
+    def digits(h, l, x):
+        aff(h, x)
+        tt(l, x, h, ALU.subtract)
+
+    def gp(fix, n, fn, R, Wr):
+        return op("g", ("g", fix, 2 * n), fn, R, Wr)
+
+    def gw(out, win, off, other=None, alu=None, ext=()):
+        s = M // NCH
+        for c in range(NCH):
+            gather(out, win, (off, 0), s * c, s * (c + 1), other, alu, ext)
+
+    for c0, src in ((PAI, T.par), (SDI, T.side), (HDI, T.heads)):
+        a = A("ints", c0, c0 + (MI if c0 == HDI else M))
+        dma(a[0], src[:], [], [a], q="sa", lat="small")
     for j in range(4):
         a = A("un", 768 * j, 768 * (j + 1))
-        dma(a[0], T.cnt[:, 768 * j:768 * (j + 1)], [], [a], q="s", lat=3.0 + 0.9 * j)
-    for r in range(N):
-        a = A("hdi", 8 * r, 8 * r + 8)
-        dma(a[0], T.heads[:, 128 * r:128 * (r + 1)], [], [a], q="a", lat=3.5)
-    for nm, src in (("bti", T.bit), ("iti", T.itm)):
-        dma(T[nm][:], src[:], [], [A(nm)], q="s", lat=5.0)
-    dma(T.thi[:, 0:1], T.th[:], [], [A("thi")], q="s", lat=5.0)
+        dma(a[0], T.cnt[:, 768 * j:768 * (j + 1)], [], [a], q="sa", lat="cnt%d" % j)
+    for c0, src in ((ITI, T.itm), (BTI, T.bit)):
+        a = A("ints", c0, c0 + M)
+        dma(a[0], src[:], [], [a], q="sa", lat="late")
+    dma(T.thi[:, 0:1], T.th[:], [], [A("thi")], q="sa", lat="late")
 
-    mset(A("wv"), 0.0)
+    mset(A("zz"), 0.0)
     mset(A("ones"), 1.0)
-    gp(0.2, lambda e: g.iota(T.pi[:, 0:1], [[0, 1]], 0, 1), [], [A("pi", 0, 1)])
-    gp(0.5, lambda e: g.iota(T.mf[:], [[1, M]], 0, 0, allow_small_or_imprecise_dtypes=True), [], [A("mf")])
+    gp(0.13, 1, lambda e: g.iota(T.pi[:, 0:1], [[0, 1]], 0, 1), [], [A("pi", 0, 1)])
+    gp(0.13, M, lambda e: g.iota(T.mf[:], [[1, M]], 0, 0, allow_small_or_imprecise_dtypes=True), [], [A("mf")])
+    zero("wv", 0, 144 * len(WV))
+    zero("tab", 0, 2 * W)
+    zero("pt", 0, W)
     for v, rows in WV.items():
         a = A("wv", WOFF[v] + 15, WOFF[v] + 143, 16)
         if rows is None:
             mset(a, 16384.0)
-            gp(0.2, lambda e, a=a: g.affine_select(a[0], a[0], [[-16, 8]], ALU.is_ge, 0.0, 0, 1), [a], [a])
-            gp(0.2, lambda e, a=a: g.affine_select(a[0], a[0], [[16, 8]], ALU.is_ge, 0.0, 15, -1), [a], [a])
+            gp(0.17, 8, lambda e, a=a: g.affine_select(a[0], a[0], [[-16, 8]], ALU.is_ge, 0.0, 0, 1), [a], [a])
+            gp(0.17, 8, lambda e, a=a: g.affine_select(a[0], a[0], [[16, 8]], ALU.is_ge, 0.0, 15, -1), [a], [a])
         else:
             for r, w in rows.items():
-                gp(0.2, lambda e, a=a, r=r, w=w: g.affine_select(a[0], a[0], [[-16, 8]], ALU.not_equal, float(w), -r, 1), [a], [a])
-    gp(0.4, lambda e: g.affine_select(T.idn[:], T.ones[:], [[-1, 128]], ALU.is_equal, 0.0, 0, 1), [A("ones")], [A("idn")])
-    gp(0.4, lambda e: g.affine_select(T.bo[:], T.ones[:], [[-16, 8], [0, 16]], ALU.is_ge, 0.0, 0, 1), [A("ones")], [A("bo")])
-    gp(0.4, lambda e: g.affine_select(T.bo[:], T.bo[:], [[16, 8], [0, 16]], ALU.is_ge, 0.0, 15, -1), [A("bo")], [A("bo")])
-    aff(A("id3"), A("idn"), 3072.0)
-    for nm, c0 in (("pt", 0), ("tab", 2 * W)):
-        for c in range(3):
-            a = A(nm, c0 + I * c, c0 + I * (c + 1))
-            gp(1.9, lambda e, a=a: g.iota(a[0], [[0, I]], 0, 0, allow_small_or_imprecise_dtypes=True), [], [a])
+                gp(0.17, 8, lambda e, a=a, r=r, w=w: g.affine_select(a[0], a[0], [[-16, 8]], ALU.not_equal, float(w), -r, 1), [a], [a])
+    gp(0.17, 128, lambda e: g.affine_select(T.idn[:], T.ones[:], [[-1, 128]], ALU.is_equal, 0.0, 0, 1), [A("ones")], [A("idn")])
+    gp(0.17, 128, lambda e: g.affine_select(T.bo[:], T.ones[:], [[-16, 8], [0, 16]], ALU.is_ge, 0.0, 0, 1), [A("ones")], [A("bo")])
+    gp(0.17, 128, lambda e: g.affine_select(T.bo[:], T.bo[:], [[16, 8], [0, 16]], ALU.is_ge, 0.0, 15, -1), [A("bo")], [A("bo")])
+    aff(A("nid"), A("idn"), -1.0)
     ts(A("pi", 1, 2), A("pi", 0, 1), 15, None, ALU.bitwise_and)
-    cq, cq192, cnz, cz, cth, cb, cq3 = [A("col", i, i + 1) for i in range(7)]
+    cq, cq192, cq3, cnz, cz, cth, ck, csg, ctr, cd = [A("col", i, i + 1) for i in range(10)]
     aff(cq, A("pi", 1, 2))
     aff(cq192, cq, 192.0)
-    aff(cq3, cq, 1.0, 3072.0)
+    aff(cq3, cq, 192.0, 3072.0)
     ts(cnz, cq, 0.5, None, ALU.is_ge)
-    aff(cz, cnz, -1024.0, 1024.0)
-    aff(cb, cnz, -1e6, 1e6)
+    aff(cz, cnz, -float(KEPT), float(KEPT))
+    ts(ck, cq, 3.5, None, ALU.is_lt)
+    aff(csg, ck, 2.0, -1.0)
+    aff(ctr, ck, 1.0, -0.5)
+    aff(cd, ck, -1.0, 1.0)
     aff(cth, A("thi", 0, 1))
-    mset(A("att"), 0.0)
-    mset(A("tab", 0, W), 0.0)
-    mset(A("tab", W, 2 * W), 0.0)
-    mset(A("un", W, W + 16), 0.0)
+    if PRE[0] or PRE[1]:
+        ts(A("col", 10, 11), cq, float(NX), 128.0, ALU.is_equal, ALU.mult)
+        ts(A("f128"), A("bo"), A("col", 10, 11), None, ALU.mult)
     mset(A("one"), 1.0)
-    mset(A("twos"), 2.0)
+    mset(A("l3", W, W + 16), -1.0)
     for t in range(2):
-        mset(A("kt%d" % t, I, I + 16), 0.5)
-    ts(A("nf"), A("mf"), cq192, None, ALU.add)
-    ts(A("sf3"), A("mf"), 16.0, cq3, ALU.mult, ALU.add)
-    ts(A("idq"), A("mf"), 0.0, cq, ALU.mult, ALU.add)
+        aff(A("kt%d" % t, I, I + 16), A("zz", 0, 16), 1.0, cd)
+        aff(A("kt%d" % t, KEPT, KEPT + 1), ck)
+    aff(A("idq"), A("zz", 0, M), 1.0, cq192)
+    aff(A("idq3"), A("zz", 0, M), 1.0, cq3)
     aff(A("idm"), A("mf"))
-    digits("nh", "nl", "nf")
 
-    aff(A("paf"), A("pai"))
-    aff(A("sdf"), A("sdi"))
-    digits("pah", "pal", "paf")
-    digits("sdh", "sdl", "sdf")
-    for row, src in ((PA, "pah"), (PA + 1, "pal"), (SD, "sdh"), (SD + 1, "sdl"), (ID, "idq"), (ID + 1, "idm")):
-        torow("att", row, 0, src)
-    aff(A("pa3"), A("paf"), 1.0, 3072.0)
-    torow("tab", SD, 0, "sdh")
-    torow("tab", SD + 1, 0, "sdl")
-    aff(A("ow", 0, MI), A("hdi"))
-    aff(A("hdf"), A("hdi"))
-    g2("gu1", A("att"), "ow")
-    aff(A("h3"), fold(sig("pa", "gu1", 0)), 1.0, 3072.0)
-    aff(A("hs"), fold(sig("sd", "gu1", 0)))
-    aff(A("osh"), fold(sig("sg", "gu1", 0)))
+    digits(A("hi", 0, ITI), A("lo", 0, ITI), A("ints", 0, ITI))
+    for row, c0 in ((RB, PAI), (SD, SDI)):
+        torow("tab", row, 0, A("hi", c0, c0 + M), "sa")
+        torow("tab", row + 1, 0, A("lo", c0, c0 + M), "sa")
+    for row, x in enumerate(("hi", "lo")):
+        for h in range(NH):
+            o, i = A("tab", W + I // NH * h, W + I // NH * (h + 1), row=row), A(x, HDI, HDI + MI)
+            dma(o[0], T[x][h::NH, HDI:HDI + MI], [i], [o], q="sa")
+    for row in (RA, RC):
+        torow("tab", row, 0, A("idq"), "sa")
+        torow("tab", row + 1, 0, A("idm"), "sa")
+    aff(A("pa3"), A("ints", PAI, PAI + M), 1.0, 3072.0)
+    aff(A("sdf"), A("ints", SDI, SDI + M))
+    b = fold(strided("id", "tab", W, W + I))
+    aff(A("ow", 0, MI), b)
+    aff(A("hdf"), b)
 
-    def nxt(pv, sdn):
-        tt(A("xx"), pv, A("pa3"), ALU.min)
-        tt(A("nx0"), A("xx"), A(sdn), ALU.max)
-        digits("n0h", "n0l", "nx0")
-        digits("n1h", "n1l", "xx")
-        torow("tab", NX, 0, "n0h")
-        torow("tab", NX + 1, 0, "n0l")
-        torow("tab", NX, W, "n1h")
-        torow("tab", NX + 1, W, "n1l")
+    def nxt(pv, sdn, parts=((0, M),)):
+        for c0, c1 in parts:
+            xx, n0 = A(pv[1], M + c0, M + c1), bank(c1 - c0)
+            tt(xx, A(pv[1], c0, c1), A("pa3", c0, c1), ALU.min)
+            tt(n0, xx, A(sdn, c0, c1), ALU.max)
+            digits(A("n0h", c0, c1), A("n0l", c0, c1), n0)
+            digits(A("n1h", c0, c1), A("n1l", c0, c1), xx)
+        torow("tab", NX, 0, A("n0h"), "sa")
+        torow("tab", NX + 1, 0, A("n0l"), "sa")
+        torow("tab", NX, W, A("n1h"), "sa")
+        return torow("tab", NX + 1, W, A("n1l"), "sa")
+
+    for h in range(2):
+        gather("gu1", A("tab", 0, W), ("ow", 0), 32 * h, 32 * h + 32)
+    aff(A("h3"), fold(strided("pa", "gu1", 0, I)), 1.0, 3072.0)
+    aff(A("hs"), fold(strided("sd", "gu1", 0, I)))
+    aff(A("osh"), fold(strided("sg", "gu1", 0, I)), 1.0, 0.25)
+    ts(A("ints", ITI, ITI + 1), A("ints", ITI, ITI + 1), cnz, cz, ALU.mult, ALU.add)
+    digits(A("hi", ITI, BTI), A("lo", ITI, BTI), A("ints", ITI, BTI))
+    torow("tab", IT, 0, A("hi", ITI, BTI), "sa")
+    torow("tab", IT + 1, 0, A("lo", ITI, BTI), "sa")
+    aff(A("r1"), A("ints", BTI, BTI + M))
+    aff(A("r0"), A("r1"), -1.0, 1.0)
+    aff(A("nbf"), A("r0"))
+    for r in ("r0", "r1"):
+        ts(A(r, 0, 1), A(r, 0, 1), cnz, None, ALU.mult)
+    torow("tab", R1, 0, A("r1"), "sa")
+    torow("tab", R0, 0, A("r0"), "sa")
 
     pv = bank(M)
     for j in range(4):
         ge4(A("ge", 768 * j, 768 * (j + 1)), A("un", 768 * j, 768 * (j + 1)))
-        mm(pv, nat("vv", "ge", range(4 * j, 4 * j + 4)), j == 0, j == 3)
-    nxt(pv, "sdf")
-
-    aff(A("opa"), A("pai"))
-    aff(A("osd"), A("sdi"))
-    aff(A("btf"), A("bti"))
-    aff(A("th0"), A("btf"), 1e6)
-    aff(A("th1"), A("btf"), -1e6, 1e6)
-    aff(A("ro0"), A("btf"), 2.0)
-    aff(A("ro1"), A("btf"), -2.0, 2.0)
-    for t in range(2):
-        ts(A("th%d" % t, 0, 1), A("th%d" % t, 0, 1), cb, None, ALU.max)
-        ts(A("ro%d" % t, 0, 1), A("ro%d" % t, 0, 1), cnz, None, ALU.mult)
-    ts(A("xj"), A("iti"), 896, None, ALU.bitwise_and)
-    ts(A("xk"), A("iti"), 3, 15, ALU.logical_shift_right, ALU.bitwise_and)
-    ts(A("x3"), A("iti"), 7, None, ALU.bitwise_and)
-    aff(A("t1"), A("x3"), 16.0)
-    tt(A("t2"), A("xj"), A("xk"), ALU.add)
-    tt(A("itf"), A("t1"), A("t2"), ALU.add)
-    ts(A("itf", 0, 1), A("itf", 0, 1), cnz, cz, ALU.mult, ALU.add)
-    digits("ith", "itl", "itf")
-    aff(A("oit"), A("itf"))
-    torow("att", IT, 0, "ith")
-    torow("att", IT + 1, 0, "itl")
-    for q in range(16):
-        aff(A("us", q, W, 16), A("un", M * q, M * (q + 1)))
+        mm(pv, blocks("vv", "ge", range(4 * j, 4 * j + 4)), j == 0, j == 3)
+    ld = nxt(pv, "sdf")
+    for j in range(2):
+        a = A("uc", 1536 * j, 1536 * (j + 1))
+        dma(a[0], T.cnt[:, a[2]:a[3]], [], [a], lat="big", ext=[ld])
+    aff(A("opa"), thirds("pa", "tab"))
+    b = thirds("sd", "tab")
+    aff(A("osd"), b)
+    aff(A("sdt"), b)
+    tt(A("osc"), thirds("nsd", "tab", [("idn", "idq3"), ("idn", "idm")]), A("sdt"), ALU.max)
 
     others = [r for r in range(N) if r != rank]
     eng = topo.engines(core, T.cores[others[0]])
@@ -349,193 +376,251 @@ def build(g, T, topo, core, rank):
         a = topo.addr(T.cores[r])
         return DstId(rid=a[0], pnc=a[1])
 
+    def remote(tr, src, kind, first):
+        k = op("g", ("r",), lambda e: g.remote_dma_fused(tr, local_sem=T.sem.loc), [src], [], lat="first" if first else None, kind=kind)
+        return op("w", ("w", 1.0 / NH), lambda e: None, [src], [], lat="fly", kind="w", ext=[k])
+
     def walk(t):
-        nb[1] = 6
-        acc = [A("ps6"), A("ps7")]
+        acc = [bank(512), bank(512)]
         S = lambda n, s: A(n, MI * s, MI * (s + 1))
         for s in range(4):
-            gw = "gw%d" % (s % 2)
-            if s == 0:
-                g2(gw, A("ge"), "ow")
-                tt(A("hx"), fold(sig("vv", gw, 0)), A("h3"), ALU.min)
-                pn, prev = A("hx"), A("hs")
-            else:
-                g2(gw, A("tab", 0, 2 * W), "ow", MI * s)
-                pn, prev = fold(sig("nx", gw, 0)), S("sck", s - 1)
-            if s < 3:
-                if TTU:
-                    tt(S("ow", s + 1), pn, prev, ALU.max)
-                    tt(S("wf", s), pn, prev, ALU.max)
-                else:
-                    tt(S("wf", s), pn, prev, ALU.max)
-                    aff(S("ow", s + 1), S("wf", s))
-            ts(S("nf3", s), pn, 3072.0, 3072.0, ALU.is_ge, ALU.mult)
-            if s == 0:
-                tt(S("sck", 0), A("hs"), S("nf3", 0), ALU.min)
-            elif s == 1:
-                tt(S("sc", 1), fold(sig("sd", gw, 0)), S("sck", 0), ALU.add)
-                tt(S("sck", 1), S("sc", 1), S("nf3", 1), ALU.min)
-            ttu(S("om", s), S("wm", s), A("hdf") if s == 0 else S("wn", s - 1), S("nf3", s), ALU.min)
-            if s < 3:
-                tt(S("wn", s), S("wf", s), S("nf3", s), ALU.subtract)
+            gwn = "gw%d" % (s % 2)
             for h in range(2):
-                gather("gu%d" % s, A("un", 0, W), ("om", MI * s), 32 * h, 32 * h + 32)
-                mm(acc[h], [(A("idn"), A("gu%d" % s, 512 * h, 512 * h + 512))], s == 0, s == 3)
+                gather(gwn, A("ge") if s == 0 else A("tab"), ("ow", MI * s), 32 * h, 32 * h + 32)
+            if s == 0:
+                b = fold(strided("vv", gwn, 0, I))
+                pn, prev = A(b[1], 128, 192), A("hs")
+                tt(pn, b, A("h3"), ALU.min)
+            else:
+                pn, prev = fold(strided("nx", gwn, 0, I)), S("sck", s - 1)
+            nf = A(pn[1], 64, 128)
+            if s < 3:
+                tt(S("ow", s + 1), pn, prev, ALU.max)
+                tt(S("wf", s), pn, prev, ALU.max)
+            ts(nf, pn, 3072.0, 3072.0, ALU.is_ge, ALU.mult)
+            if s == 0:
+                tt(S("sck", 0), nf, A("hs"), ALU.min)
+            elif s == 1:
+                tt(S("sc", 1), fold(strided("sd", gwn, 0, I)), S("sck", 0), ALU.add)
+                tt(S("sck", 1), nf, S("sc", 1), ALU.min)
+            tt(S("om", s), A("hdf") if s == 0 else S("wn", s - 1), nf, ALU.min)
+            if s < 3:
+                tt(S("wn", s), S("wf", s), nf, ALU.subtract)
+            for h in range(2):
+                k = gather("gu%d" % s, A("un"), ("om", MI * s), 32 * h, 32 * h + 32, clamp=t == 1)
+                pick = (lambda k=k: T.nid[:] if where[k] == "a" else T.idn[:]) if t == 1 else None
+                mm(acc[h], [(A("nid" if t == 1 else "idn"), A("gu%d" % s, 512 * h, 512 * h + 512))], s == 0, s == 3, pick=pick)
         snd, lnd, kt = "snd%d" % t, "lnd%d" % t, "kt%d" % t
-        for h in range(2):
-            aff(A(snd, 512 * h, 512 * h + 512), acc[h])
-        nb[1] = 8
-        tr = [RemoteDMATransfer(dst_ids=[dst(r)], dma_engine_mask=1 << eng[i], remote_sem=T.sem["rs%d" % t],
-                                src=T[snd][:, 128 * r:128 * (r + 1)], dst=T[lnd][:, 128 * rank:128 * (rank + 1)])
-              for i, r in enumerate(others)]
-        k1 = op("g", 0.5, lambda e: g.remote_dma_fused(tr, local_sem=T.sem.loc), [A(snd)], [], lat=REML, kind=("rs%d" % t, N - 1, N - 1))
-        pt_ = bank(128)
-        mm(pt_, [(A("idn"), A(snd if r == rank else lnd, 128 * r, 128 * (r + 1))) for r in range(N)], ext=[k1])
-        ts(A("gev"), pt_, cth, 0.5, ALU.is_ge, ALU.subtract)
-        pc = fold([(A("bo"), A("gev"))], 128)
-        own = A(kt, 128 * rank, 128 * (rank + 1))
-        ts(own, pc, 0.5, 0.5, ALU.is_ge, ALU.subtract)
         mask = 0
         for e_ in eng:
             mask |= 1 << e_
-        tr2 = [RemoteDMATransfer(dst_ids=[dst(r) for r in others], dma_engine_mask=mask, remote_sem=T.sem["kv%d" % t],
-                                 srcs=[own[0]], dsts=[own[0] for r in others])]
-        k2 = op("g", 0.5, lambda e: g.remote_dma_fused(tr2, local_sem=T.sem.loc), [own], [], lat=REML,
-                kind=("kv%d" % t, (N - 1) * len(eng), len(eng)))
-        aff(A("t7", 0, 128), pt_)
-        for m in range(8):
-            aff(A("yas", 128 * t + m, 128 * (t + 1), 8), A("t7", 16 * m, 16 * m + 16))
-        return k2
+        for h in range(2):
+            aff(A(snd, 512 * h, 512 * h + 512), acc[h], 1.0, 60.0 * t)
+        n, kv = 128 // NH, []
+        for h in range(NH):
+            c = I // NH * h
+            tr = [RemoteDMATransfer(dst_ids=[dst(r)], dma_engine_mask=1 << eng[i], remote_sem=T.sem["rs%d%d" % (t, h)],
+                                    src=T[snd][:, c + n * r:c + n * (r + 1)], dst=T[lnd][:, c + n * rank:c + n * (rank + 1)])
+                  for i, r in enumerate(others)]
+            k1 = remote(tr, A(snd, c, c + I // NH), ("rs%d%d" % (t, h), N - 1, N - 1), t + h == 0)
+            tot = bank(n)
+            mm(tot, [(A("idn"), A(snd if r == rank else lnd, c + n * r, c + n * (r + 1))) for r in range(N)], ext=[k1])
+            ts(A("gev", n * h, n * h + n), tot, cth, 0.5, ALU.is_ge, ALU.subtract)
+            pc = fold([(A("bo"), A("gev", n * h, n * h + n))], n)
+            own = A(kt, 128 * rank + n * h, 128 * rank + n * h + n)
+            ts(own, pc, csg, ctr, ALU.mult, ALU.is_ge)
+            tr = [RemoteDMATransfer(dst_ids=[dst(r) for r in others], dma_engine_mask=mask, remote_sem=T.sem["kv%d%d" % (t, h)],
+                                    srcs=[own[0]], dsts=[own[0] for r in others])]
+            kv.append(remote(tr, own, ("kv%d%d" % (t, h), (N - 1) * len(eng), len(eng)), False))
+            aff(A("yas", 128 * t + n * h, 128 * t + n * h + n), tot)
+        return kv
 
-    def pre_par():
-        g6("ga", A("att"), "opa")
-        aff(A("oip"), whole("it", "ga"))
-        aff(A("p2f"), whole("pa", "ga"))
+    def pre_par(t):
+        gw("ga", A("tab", 0, W), "opa")
+        aff(A("oip"), thirds("it", "ga"))
+        for r in range(2):
+            o, i = A("ga", row=RE + r), A("tab", 0, W, row=RA + r)
+            dma(o[0], i[0], [i], [o], q="sa")
+        torow("ga", NX, 0, A("one"), "sa")
+        if PRE[t]:
+            gw("sm", A("un"), "opa", "uc", ALU.add)
+
+    def partners(t):
+        ca = bank(M)
+        for j in range(3):
+            mm(CH(ca[1], j), strided("itb%d" % t, "tab", 1024 * j, 1024 * (j + 1)) + strided("r%dn" % (1 - t), "gb", 1024 * j, 1024 * (j + 1)))
+        ts(A("t1"), ca, BIG * (1 + t), float(DROP), ALU.add, ALU.min)
+        cs = thirds("itr%d" % t, "pt", [("idn", "pb%d" % (1 - t))])
+        tt(A("oit0" if t == 0 else "o1f"), cs, A("t1"), ALU.min)
+        b = thirds("id", "pt", [("nid", "pen%d" % (1 - t))])
+        tt(A("op%d" % t), b, A("sa%d" % t), ALU.max)
+        if t == 1:
+            aff(A("ox"), b)
 
     def pre_side():
-        b = fold([(wq("sd", q), A("att", q, W, 16)) for q in range(16)], M)
-        ts(A("t3"), b, 0.0, 8192.0, ALU.is_equal, ALU.mult)
-        tt(A("t4"), A("t3"), A("sf3"), ALU.min)
-        ttu(A("osc"), A("t3"), b, A("t4"), ALU.max)
         win = A("pt")
-        for c in range(12):
-            src, f = A("att", 256 * c, 256 * c + 256), A("osc", 16 * c, 16 * c + 16)
-            op("v", FIX + CY * SC * 256, lambda e, src=src, f=f: g.vector.tensor_copy(win[0].indirect(f[0]), src[0]), [src, f], [win])
-        g6("gb", A("att"), "osd")
-        aff(A("sgs"), whole("sg", "gb"))
-        tt(A("d2"), whole("sd", "gb"), A("sdf"), ALU.subtract)
-        b = fold(nat("sg", "pt"), M)
-        tt(A("t5"), b, A("sgs"), ALU.subtract)
-        tt(A("t6"), A("t5"), A("btf"), ALU.mult)
-        ttu(A("op1"), A("t5"), b, A("t6"), ALU.subtract)
-        ttu(A("op0"), A("t4"), A("sgs"), A("t6"), ALU.add)
-        ts(A("dq"), fold(nat("rq", "pt"), M), cq, None, ALU.subtract)
-        tt(A("dm"), fold(nat("rm", "pt"), M), A("mf"), ALU.subtract)
+        for c in range(W // SCH):
+            src, f = A("tab", SCH * c, SCH * c + SCH), A("osc", SCH // 16 * c, SCH // 16 * (c + 1))
+            op("v", ("sc", SCH), lambda e, src=src, f=f: g.vector.tensor_copy(win[0].indirect(f[0]), src[0]), [src, f], [win])
+        gw("gb", A("tab", 0, W), "osd")
+        b = thirds("bit", "tab")
+        aff(A("pen0"), b, BIG)
+        aff(A("pen1"), b, -BIG, BIG)
+        aff(A("pb0"), b, BIG, BIG)
+        aff(A("pb1"), b, -BIG, 2 * BIG)
+        for t in range(2):
+            tt(A("sa%d" % t), A("sdt"), A("pen%d" % t), ALU.subtract)
+        partners(0)
+        for x, v, own in (("dq", "a0", "idq"), ("dm", "a1", "idm")):
+            b = bank(M)
+            mm(b, [(A("nid"), A(own))], True, False)
+            for j in range(4):
+                mm(b, blocks(v, "pt", range(4 * j, 4 * j + 4)), False, j == 3)
+            for t in range(2):
+                tt(A("%s%d" % (x, t)), b, A("r%d" % (1 - t)), ALU.mult)
+        b = quarters("sd", "gb")
+        tt(A(b[1], M, 2 * M), b, A("nbf"), ALU.mult)
+        tt(A("ds"), A(b[1], M, 2 * M), A("sdf"), ALU.subtract)
 
     def post(t, kv):
         kt = A("kt%d" % t)
-        g6("gc2", kt, "oip", ext=[kv])
-        b = bank(M)
+        gw("a1", kt, "oip", "ga", ALU.mult, ext=kv)
+        gw("k0", kt, "oit%d" % t, ext=kv)
         for j in range(3):
-            mm(CH(b[1], j), sig("kp", "gc2", j) + [(A("idn"), CH("pah", j)), (A("idn"), CH("pal", j))])
-        tt(A("tj"), b, A("p2f"), ALU.max)
-        ts(A("opm"), b, 4096.0, 3072.0, ALU.add, ALU.min)
-        g6("gf", kt, "oit", ext=[kv])
-        for j in range(3):
-            b = fold(sig("kn", "gf", j) + [(A("idn"), CH("nh", j)), (A("idn"), CH("nl", j))])
-            tt(CH("xj", j), b, CH("tj", j), ALU.max)
-            tt(CH("eb", j), b, CH("th%d" % t, j), ALU.is_ge)
-            ts(CH("xk", j), CH("xj", j), 4095, None, ALU.bitwise_and)
-            digits("jh", "jl", "xk", 64 * j, 64 * j + 64)
-        for c0 in (0, W, 2 * W):
-            torow("tab", JJ, c0, "jh")
-            torow("tab", JJ + 1, c0, "jl")
-        g6("ua", A("un"), "opm", add="us")
-        g6("gc2", A("tab", 0, W), "opa")
-        for j in range(3):
-            aff(CH("od", j), fold(sig("jj", "gc2", j) + [(A("id3"), CH("eb", j)), (A("id3"), CH("ro%d" % t, j))]))
-        g6("gd", A("tab"), "od")
-        aff(A("oi"), whole("jj", "gd"))
-        g6("gf", A("gd"), "op%d" % t)
-        for j in range(3):
-            b = bank()
-            mm(b, sig("md", "gd", j), True, False)
-            mm(b, sig("mf", "gf", j), False, True)
-            ts(CH("mb", j), b, 28672.0, None, ALU.is_equal)
-            ts(CH("ma", j), b, 20480.0, None, ALU.is_equal)
-            tt(CH("deh", j), CH("mb", j), CH("dq", j), ALU.mult)
-            tt(CH("del", j), CH("mb", j), CH("dm", j), ALU.mult)
-            ttu(CH("osm", j), CH("t1", j), CH("ma", j), CH("sgs", j), ALU.mult)
-        torow("tab", DL, 0, "deh")
-        torow("tab", DL + 1, 0, "del")
-        if t == 0:
-            tt(A("t2"), A("ma"), A("d2"), ALU.mult)
-            aff(A("t3"), A("mb"), 1e6)
-            tt(A("t4"), A("t2"), A("sdf"), ALU.add)
-            tt(A("t5"), A("t4"), A("t3"), ALU.subtract)
-            relu(A("sd1"), A("t5"))
-            digits("sdh", "sdl", "sd1")
-            tt(A("th1"), A("t3"), A("th1"), ALU.max)
-            torow("att", SD, 0, "sdh")
-            torow("att", SD + 1, 0, "sdl")
-            g2("gu1", A("att"), "ow")
-            aff(A("hs"), fold(sig("sd", "gu1", 0)))
-        g6("ub", A("ua"), "osm")
-        for q in range(1, 16, 2):
-            b = bank(2 * M)
-            for h in range(2):
-                mm(A(b[1], M * h, M * h + M), [(A("idn"), A(x, q - 1 + h, W, 16)) for x in ("ua", "ub")])
-            ts(A("un", M * (q - 1), M * (q + 1)), b, 15.0, None, ALU.min)
-            if q % 4 == 3:
-                a = A("un", M * (q - 3), M * (q + 1))
-                if t == 0:
-                    ge4(A("ge", a[2], a[3]), a)
-                else:
-                    dma(T.yc[:, a[2]:a[3]], a[0], [a], [], lat=3.0)
-        g6("gc2", A("tab", 0, W), "oi")
-        if t == 0:
-            torow("tab", SD, 0, "sdh")
-            torow("tab", SD + 1, 0, "sdl")
-            g2("gu2", A("gc2"), "osh")
-            aff(A("h3"), fold(sig("rp", "gu2", 0)), 1.0, 3072.0)
-            b = whole("rp", "gc2")
-            aff(A("pa3"), b, 1.0, 3072.0)
-            aff(A("paf"), b)
-            pv = bank(M)
-            for j in range(4):
-                mm(pv, nat("vv", "ge", range(4 * j, 4 * j + 4)), j == 0, j == 3)
-            nxt(pv, "sd1")
-            aff(A("opa"), A("paf"))
-            digits("pah", "pal", "paf")
-            torow("att", PA, 0, "pah")
-            torow("att", PA + 1, 0, "pal")
+            if PRE[t]:
+                aff(CH("o2", j), fold(strided("nxs", "a1", 1024 * j, 1024 * (j + 1))))
+                continue
+            b = fold(strided("nxd", "a1", 1024 * j, 1024 * (j + 1)))
+            ts(CH("t3", j), b, 4096.0, -4096.0, ALU.is_ge, ALU.mult)
+            tt(CH("o2", j), b, CH("t3", j), ALU.add)
+            aff(CH("opm", j), b, 1.0, -4096.0)
+        tt(A("opk"), thirds("kd", "k0"), A("op%d" % t), ALU.max)
+        gw("l2", A("a1"), "o2")
+        if PRE[t]:
+            for c in range(6):
+                b = fold([(A("idn"), A("un", 512 * c, 512 * c + 512)), (A("f128"), A("a1", 512 * c, 512 * c + 512))], 512)
+                tt(A("ua", 512 * c, 512 * c + 512), b, A("sm", 512 * c, 512 * c + 512), ALU.min)
         else:
-            aff(A("ypf"), whole("rp", "gc2"))
-            dma(T.yp[:], T.ypf[:], [A("ypf")], [])
+            gw("ua", A("un"), "opm", "uc", ALU.add)
+        for c in range(G6A[t], 6):
+            o, i = A("ub", 512 * c, 512 * c + 512), A("ua", 512 * c, 512 * c + 512)
+            dma(o[0], i[0], [i], [o], lat="out")
+        for j in range(3):
+            aff(CH("o3", j), fold(strided("nxs", "l2", 1024 * j, 1024 * (j + 1))))
+        gw("l3", A("l2"), "o3")
+        bt = [bank() for j in range(3)]
+        for j in range(3):
+            mm(bt[j], strided("nval", "l3", 1024 * j, 1024 * (j + 1)), True, False)
+        b = quarters("val", "l3")
+        aff(A("p1f"), b)
+        aff(A("oi"), b)
+        gw("g5", A("l3"), "opk")
+        b = quarters("val", "g5")
+        hit = A(b[1], M, 2 * M)
+        tt(hit, b, A("p1f"), ALU.is_equal)
+        tt(A("deh"), hit, A("dq%d" % t), ALU.mult)
+        tt(A("del"), hit, A("dm%d" % t), ALU.mult)
+        torow("tab", RE, 0, A("deh"), "sa")
+        torow("tab", RE + 1, 0, A("del"), "sa")
+        for j in range(3):
+            mm(bt[j], strided("val", "g5", 1024 * j, 1024 * (j + 1)), False, True)
+            hb = A(bt[j][1], 64, 128)
+            ts(hb, bt[j], 0.0, BIG, ALU.is_equal, ALU.mult)
+            tt(CH("osm", j), hb, CH("sa%d" % t, j), ALU.min)
+            if t == 0:
+                tt(CH("sa1", j), CH("sa1", j), hb, ALU.subtract)
+        if t == 0:
+            b = bank(M)
+            tt(b, hit, A("ds"), ALU.mult)
+            aff(A("hit"), hit)
+            torow("tab", R0, 0, A("hit"), "sa")
+            tt(A("sd1"), b, A("sdf"), ALU.add)
+            digits(A("sdh"), A("sdl"), A("sd1"))
+            torow("tab", SD, 0, A("sdh"), "sa")
+            torow("tab", SD + 1, 0, A("sdl"), "sa")
+        pv = bank(M) if t == 0 else None
+        for c in range(6):
+            a = A("un", 512 * c, 512 * (c + 1))
+            if c >= G6A[t]:
+                gather("un", A("ua"), ("osm", 0), 32 * c, 32 * c + 32, "ub", ALU.add)
+                if t == 1:
+                    ts(a, a, 15.0, None, ALU.min)
+                    dma(T.yc[:, a[2]:a[3]], a[0], [a], [], lat="out")
+                continue
+            gather("g6", A("ua"), ("osm", 0), 32 * c, 32 * c + 32)
+            b = fold([(A("idn"), A(x, a[2], a[3])) for x in ("ua", "g6")], 512)
+            if t == 0:
+                aff(a, b)
+            else:
+                ts(a, b, 15.0, None, ALU.min)
+                dma(T.yc[:, a[2]:a[3]], a[0], [a], [], lat="out")
+        if t == 0:
+            for j in range(4):
+                ge4(A("ge", 768 * j, 768 * (j + 1)), A("un", 768 * j, 768 * (j + 1)))
+                mm(pv, blocks("vv", "ge", range(4 * j, 4 * j + 4)), j == 0, j == 3)
+            for h in range(2):
+                gather("gu1", A("tab", 0, W), ("ow", 0), 32 * h, 32 * h + 32)
+            aff(A("hs"), fold(strided("sd", "gu1", 0, I)))
+        gw("g7", A("tab", 0, W), "oi")
+        for j in range(3):
+            b = fold(strided("rp", "g7", 1024 * j, 1024 * (j + 1)))
+            if t == 0:
+                aff(CH("pa3", j), b, 1.0, 3072.0)
+                digits(CH("pah", j), CH("pal", j), b)
+            else:
+                aff(CH("ypf", j), b)
+        if t == 0:
+            for h in range(2):
+                gather("gu2", A("g7"), ("osh", 0), 32 * h, 32 * h + 32)
+            aff(A("h3"), fold(strided("rp", "gu2", 0, I)), 1.0, 3072.0)
+            nxt(pv, "sd1", ((0, 128), (128, M)))
+            torow("tab", RB, 0, A("pah"), "sa")
+            ld = torow("tab", RB + 1, 0, A("pal"), "sa")
+            for j in range(2):
+                o, i = A("uc", 1536 * j, 1536 * (j + 1)), A("un", 1536 * j, 1536 * (j + 1))
+                dma(o[0], i[0], [i], [o], lat="big", ext=[ld])
+        else:
+            dma(T.yp[:], T.ypf[:], [A("ypf")], [], q="sa")
 
     kv = walk(0)
-    torow("tab", ID, 0, "idq")
-    torow("tab", ID + 1, 0, "idm")
-    torow("tab", FL, W, "one")
-    torow("tab", FL, 2 * W, "twos")
-    pre_par()
+    pre_par(0)
     pre_side()
     post(0, kv)
     kv = walk(1)
     dma(T.ya[:], T.yas[:], [A("yas")], [])
-    for q in range(16):
-        aff(A("us", q, W, 16), A("un", M * q, M * (q + 1)))
-    pre_par()
+    aff(A("opa"), thirds("pa", "tab"))
+    partners(1)
+    pre_par(1)
+    gw("g5", A("tab", 0, W), "ox")
+    tt(A("oit1"), thirds("h", "g5"), A("o1f"), ALU.max)
     post(1, kv)
     return ops
 
 
 def plan(ops):
-    if ORDER.strip():
-        order = [(int(w[:-1], 16), w[-1], 0.0) for w in ORDER.split()]
-        assert sorted(k for k, _, _ in order) == list(range(len(ops)))
-        return order, 0.0
-    return [(k, o["engs"][k % len(o["engs"])], 0.0) for k, o in enumerate(ops)], 0.0
+    order = [(int(w[:-1], 16), w[-1]) for w in ORDER.split()]
+    assert sorted(k for k, _ in order) == list(range(len(ops)))
+    return order
+
+
+def banks(ops, order):
+    users = {}
+    for i, (k, _) in enumerate(order):
+        for b in ops[k]["banks"]:
+            users.setdefault(b, []).append((i, k))
+    place, extra = {}, {}
+    tenant = [None] * 8
+    for i, (k, _) in enumerate(order):
+        for b in ops[k]["banks"]:
+            if b not in place:
+                last = [users[x][-1][0] if x else -1 for x in tenant]
+                p = last.index(min(last))
+                if last[p] >= i:
+                    return None, None
+                extra.setdefault(k, []).extend(j for _, j in users.get(tenant[p], []))
+                tenant[p] = b
+                place[b] = p
+    return place, extra
 
 
 def rank_program(g, core, T, topo):
@@ -543,15 +628,23 @@ def rank_program(g, core, T, topo):
     if rank is None:
         return
     ops = build(g, T, topo, core, rank)
-    order, _ = plan(ops)
+    order = plan(ops)
+    place, extra = banks(ops, order)
+    ops = build(g, T, topo, core, rank, place)
+    for k, js in extra.items():
+        for j in js:
+            ops[k]["deps"][j] = True
     queue = {"v": g.vector, "a": g.scalar, "p": g.tensor, "s": g.sync, "g": g}
     count = {"cv": 0, "ca": 0, "cp": 0, "cg": 0, "loc": 0}
     done, where = {}, {}
     seen = {e: {} for e in queue}
     nd = 0
-    for k, e, _ in order:
+    for k, e in order:
         o = ops[k]
         assert e in o["engs"]
+        if e == "w":
+            where[k], done[k] = e, done[max(o["deps"])]
+            continue
         need = {}
         for j, hard in o["deps"].items():
             if where[j] == e and ops[j]["kind"] == "c" and o["kind"] == "c" and (e == "p" or not hard):

from concourse.bass import DstId, RemoteDMATransfer
from concourse.mybir import AluOpType as ALU, ActivationFunctionType as AF

W, M, I, MI = 3072, 192, 1024, 64
BF, F, I32, U16 = "bfloat16", "float32", "int32", "uint16"
RA, RE, RC, RB, IT, R1, R0, SD, NX = 0, 2, 4, 6, 8, 10, 11, 12, 14
KEPT, DROP, BIG = I, I + 8, 8192.0
WV = {"vv": None, "id": {0: 1, 1: 1}, "nx": {14: 1, 15: 1}, "sd": {12: 1, 13: 1}, "pa": {6: 1, 7: 1},
      "nsd": {12: -8192, 13: -8192}, "it": {8: 1, 9: 1}, "bit": {10: 1}, "itb0": {8: 1, 9: 1, 10: BIG}, "itb1": {8: 1, 9: 1, 10: -BIG},
      "r1n": {10: -BIG}, "r0n": {11: -BIG}, "itr0": {8: 1, 9: 1, 11: -BIG}, "itr1": {8: 1, 9: 1, 10: -BIG},
      "a0": {0: 1}, "a1": {1: 1}, "nxd": {2: 1, 3: 1, 4: 1, 5: 1, 14: 4096}, "nxs": {2: 1, 3: 1, 4: 1, 5: 1},
      "val": {0: 1, 1: 1, 6: 1, 7: 1}, "nval": {0: -1, 1: -1, 6: -1, 7: -1}, "kd": {4: W},
      "rp": {0: 1, 1: 1, 2: 1, 3: 1}, "h": {11: DROP}, "sg": {0: 1 / 192, 1: 16}}
WOFF = {k: 144 * i for i, k in enumerate(WV)}

SCRATCH = {}


def _sb(names, cols, dty):
    for n in names.split():
        SCRATCH[n] = ("sbuf", [128, cols], dty)


_sb("tab pt", 2 * W, BF)
_sb("un uc ua ub sm ge ga gb a1 k0 l2 g5 g6 g7", W, BF)
_sb("l3", W + 16, BF)
_sb("wv", 144 * len(WV), BF)
_sb("idn nid bo f128 ones gev", 128, BF)
_sb("zz", 512, BF)
_sb("kt0 kt1", I + 16, BF)
_sb("snd0 snd1 lnd0 lnd1 gw0 gw1 gu0 gu1 gu2 gu3", I, BF)
_sb("yas", 256, F)
_sb("ints", 4 * M + MI, I32)
_sb("hi lo", 3 * M + MI, BF)
_sb("pi", 4, I32)
_sb("thi", 4, I32)
_sb("col", 12, F)
_sb("mf pa3 sdf sd1 sdt sa0 sa1 o1f t1 t3 ds ypf nbf op0 op1 p1f", M, F)
_sb("idq idm idq3 r0 r1 pen0 pen1 pb0 pb1 n0h n0l n1h n1l dq0 dm0 dq1 dm1 hit deh del sdh sdl pah pal one", M, BF)
_sb("opa osd osc oip opm o2 o3 oi opk oit0 oit1 ox osm", M, U16)
_sb("ow om", 4 * MI, U16)
_sb("hdf h3 hs", MI, F)
_sb("osh", MI, U16)
_sb("wf sck sc wn", 4 * MI, F)
for _b in range(8):
    SCRATCH["ps%d" % _b] = ("psum", [128, 512], F)

NDMA = 76
SEMAPHORES = ["cv", "ca", "cp", "cg", "loc"] + [s + x for s in ("rs", "kv") for x in ("00", "01", "10", "11")] + ["d%d" % i for i in range(NDMA)]
PAI, SDI, HDI, ITI, BTI = 0, M, 2 * M, 2 * M + MI, 3 * M + MI
NCH = 6
NH = 2
SCH = 256
G6A = (2, 3)
PRE = (0, 1)
ORDER = """
1s 2s av cg 0a 64v 6s dg 3a ev 8a 1cv fa 65v 15a 18a 27v 17v 79v 68v 66v 77a 5s 1bv 19g 7av 7bv 7s 1ag 16a 9s 81a 4s 80s 84s 86s a1a 20v 2ag 2bg 83a 89v 82s 88v 7es 7fs 28g 7ds 29g 2cg 1da 69a a2p a3v a4p 95v 14a 1fg 87s 9av 9bv 96v 1eg 97v a5a 2dg 2eg 9ev 30g 8ap 67v a7a 85s 25g a6p bv 7cs 34g 8bv 8dv 31g a8p a9v 9ca 9dv aav adv 8ea 99s a0s 8fp 98s 2fg 91p 6ev 60g b1s 5eg 5fg c3a 11g 32g 33g aba afs 23g aev acv b2s c2a c4p 63v 143p 13cp 8ca 10v 36g 92v 37g 61g 22v 21v 9fs 78v b0s 90a c5v c6v 12a 46g c7v 26g b4s 24a 13a 58g 3dg 6av 47g 93p 54g b9p bap 55g c8v c9v cav 6dv d0a 50g d1v 4cg 4dg 73a 38g ccv 75a 62g cea 74a d2p bbp 6fv 3ag d3v dfa d4v 39g 56g 35g 48g 6ba b3s 76a e0v 6ca bcv bda 42g 3fg d6p d5v d7v cbv d8v d9v dav 4eg e1p e2v 49g 51g bep 59g 40g 4ag bfp c0p 45g 52g e3v 57g 41g 3bg 71v 121a e4v 5dg ebv 43g 5ag e5v e6v cfp 44g 5bg dba cdp dcp eca edp e7v c1v 127p b5p b6p b7p 70v 53g 123a dda 115v dep e9a eap eev 94v efv f2a 4bg 116v 3cg f0a f3p 72v f5a 117v e8p f1p f4a b8v 118v 119v 11av 128p 129p 4fg 11bv 11cv ffg 100w 122a 14ap 14bp 125a 12aa 130p f6g f7w 5cg 124a 131p 126a 109a 10ba 101p 102v 107a 10ca 11dv 132p 103p 104v 105g 106w 108a 14cp 14dp 11ev 10aa f8p f9v fap fbv fcg 11fv 120v 10da 10ep 10fp 110p 112s 12ba 12fv 3eg 14ev 14fv 111v 133v 12ca 12da 134p 12ev 135p 136p 137v fdw 114a 113s 154v 138p 139p 144p 145p 155v 159a 156a 15ba 151v 157a 153v 13dp 150v 13ep fea 164p 165v 13fp 140p 13ap 158a 152v 166v 167v 15aa 15cp 15dv 15ev 13bv 170a 160p 161v 247p 162v 176v 171a 180p 17as 177v 17bs 243p 168p 169p 16ap 141v 163v 174v 16ca 16fa 175v 15fv 178s 181v 16da 16ea 186a 248p 179s 173v 17ep 17fv 184v 244p 17cp 146p 147p 187a 17dv 183v 185a 189p 148v 16bv 182a 18bp 18cp 18dp 194v 193a 192v 191a 195a 172v 196a 1a4p 1a5v 1a6v 1a7v 1bbv 18ep 18fa 190v 197p 198p 199p 19ap 19bv 19cv 19dv 19fa 1acv 19es 1ada 188p 1a0p 1a1v 18ap 1afv 1a2v 1a3v 1bav 1b0a 1b2s 1b7a 1a8p 1a9v 1aav 1b1v 1bdv 1bcv 1b4a 1b8p 1b9a 1abv 1b5p 1b6a 1bev 245p 1c2v 1b3s 1aes 1cav 1cev 249p 1ccv 1bfp 1c0a 1c1p 1c3p 1cfv 1c4a 1c5p 1cba 1cda 1c7a 1d0p 1d1v 1d4p 1d5v 1f5a 1dcv 1e0v 1d6a 1d2a 1d3v 1d8p 1c6a 1e1v 1e4v 1d7v 1e5v 1d9a 1dav 1e6v 1f0s 1e2a 1dbv 1e7v 1eav 1f1s 1ees 1dda 1e8a 1e3v 1f4a 1ecs 1ebv 1e9v 1c8p 24av 24bv 1efs 1eds 142v 1dep 149v 1dfa 1c9a 1f6p 1f7v 1f8v 203a 23bp 23cp 1f9v 1fav 1fbv 1fcv 202v 1fea 1f2s 200v 204p 205v 206v 1fdv 212a 211v 208p 209v 207v 262a 20av 20bv 20cv 23dp 20da 213p 214v 215v 21ev 216v 217v 218v 219v 23fp 21da 21fp 1f3s 1ffp 21ba 20fa 201p 20ep 220v 221v 21ap 224a 222v 223p 226a 210p 21cp 225p 23ev 25ev 227a 240p 241p 25fv 260v 265p 24ea 24da 24cv 252p 242v 246v 261a 250a 24fv 228g 229w 22ap 22bv 22cp 230a 251a 231g 264a 232w 233p 22dv 22eg 22fw 25dv 234v 263a 235p 236v 239a 23as 253p 254p 256a 258a 259v 25bv 266p 267p 255v 268v 25cv 237g 238w 272a 273a 26fa 270a 25av 257s 269v 285p 26cv 28bp 26ev 28fp 26bv 26dv 277p 26av 278v 290v 293s 27bp 279p 27av 275p 276v 280v 27fv 274a 271a 281a 28dp 27cp 27dp 282a 283a 296p 28cv 297v 284a 29da 28ev 294p 295v 29cv 29aa 298p 299v 29fa 289p 29ea 29bv 27ev 2a9a 287p 292s 2a0p 28av 2a3p 2a4p 2a5p 2a6p 286v 2aba 2aav 2aev 2adv 2b8p 2b9v 2bav 2afp 288v 2aca 2b0p 2a7a 2b1p 2b2p 2b3v 2b4v 2b5v 2c5a 291s 2b6s 2a8v 2a1p 2bbp 2bcv 2bdv 2cdv 2a2p 2bep 2bfv 2c0v 2cev 2b7a 2c9a 2d0v 2d3v 2d6v 2c1a 2c2p 2d9a 2dba 2cap 2daa 2c6p 2e0p 2d8a 2dep 2d4v 2d5s 2d7a 2d1v 2d2s 2cfs 2c3v 2c4s 2cbv 2ccs 2e1a 2c7v 2c8s 2dfa 2dcp 2ddv 2e2s
"""


def build(g, T, topo, core, rank, place=None):
    ops = []
    log = {}
    N = len(T.cores)
    where = {}

    def A(name, c0=0, c1=None, step=1, row=None):
        buf = name
        if name.startswith("ps"):
            buf = "ps%d" % (place[name] if place else 0)
        if c1 is None:
            c1 = SCRATCH[buf][1][1]
        if row is not None:
            ap = T[buf][row::16, c0:c1]
        elif step != 1:
            ap = T[buf][:, c0:c1:step]
        else:
            ap = T[buf][:, c0:c1]
        return (ap, name, c0, c1, row, len(range(c0, c1, step)), step)

    def dty(x):
        return F if x[1].startswith("ps") else SCRATCH[x[1]][2]

    def two(*a):
        return all(dty(x) in (BF, U16) for x in a)

    def op(engs, dur, fn, R, Wr, lat=None, kind="c", ext=()):
        k = len(ops)
        deps = {}
        for acc, wr in ((R, False), (Wr, True)):
            for a in acc:
                name, c0, c1, row, st = a[1], a[2], a[3], a[4], a[6]
                psum = name.startswith("ps")
                if psum:
                    c0, c1, st = 0, 512, 1
                lst = log.setdefault(name, [])
                for (j, d0, d1, drow, dwr, dst_) in lst:
                    if j == k or d1 <= c0 or c1 <= d0 or (row is not None and drow is not None and row != drow):
                        continue
                    if st > 1 and st == dst_ and (c0 - d0) % st:
                        continue
                    if dwr or wr:
                        deps[j] = True
                    elif psum:
                        deps.setdefault(j, False)
                if wr and row is None and st == 1:
                    lst[:] = [e for e in lst if not (c0 <= e[1] and e[2] <= c1)]
                lst.append((k, c0, c1, row, wr, st))
        for j in ext:
            deps[j] = True
        if not isinstance(dur, dict):
            dur = {e: dur for e in engs}

        def run(e, k=k):
            where[k] = e
            return fn(e)
        ops.append({"engs": engs, "dur": dur, "fn": run, "deps": deps, "lat": lat, "kind": kind, "tag": (Wr or R)[0][1],
                    "banks": sorted(set(a[1] for a in list(R) + list(Wr) if a[1].startswith("ps")))})
        return k

    def sc_ap(s):
        return s[0] if isinstance(s, tuple) else s

    def cyc(n, half=False):
        return ("c", max(64, n * (0.5 if half else 1)))

    def ts(out, in0, s1, s2, op0, op1=None):
        rd = [in0] + [s for s in (s1, s2) if isinstance(s, tuple)]
        if op1 is None:
            fn = lambda e: g.vector.tensor_scalar(out[0], in0[0], sc_ap(s1), None, op0)
        else:
            fn = lambda e: g.vector.tensor_scalar(out[0], in0[0], sc_ap(s1), sc_ap(s2), op0, op1)
        return op("v", cyc(out[5], two(out, in0)), fn, rd, [out])

    def tt(out, a, b, alu):
        ps = a[1].startswith("ps") or b[1].startswith("ps")
        return op("v", cyc(out[5] * (1 if ps else 2)), lambda e: g.vector.tensor_tensor(out[0], a[0], b[0], alu), [a, b], [out])

    def aff(out, in0, mul=1.0, add=0.0):
        fl = all(dty(x) in (BF, F) for x in (out, in0))
        plain = mul == 1.0 and add == 0.0
        ad = add[0] if isinstance(add, tuple) else float(add)

        def fn(e):
            if e == "a":
                if plain:
                    return g.scalar.activation(out[0], in0[0], AF.Copy)
                return g.scalar.activation(out[0], in0[0], AF.Identity, bias=ad, scale=float(mul))
            if plain:
                return g.vector.tensor_copy(out[0], in0[0])
            return g.vector.tensor_scalar(out[0], in0[0], float(mul), ad, ALU.mult, ALU.add)
        d = {"v": cyc(out[5], two(out, in0)), "a": cyc(out[5])}
        return op("va" if fl else "v", d, fn, [in0] + ([add] if isinstance(add, tuple) else []), [out])

    def ge4(out, in0):
        def fn(e):
            if e == "a":
                return g.scalar.activation(out[0], in0[0], AF.Sign, bias=-3.5)
            return g.vector.tensor_scalar(out[0], in0[0], 4.0, 0.5, ALU.is_ge, ALU.subtract)
        return op("va", {"v": cyc(out[5], True), "a": cyc(out[5])}, fn, [in0], [out])

    def mset(out, val):
        return op("v", cyc(out[5], two(out)), lambda e: g.vector.memset(out[0], val), [], [out])

    def zero(name, c0, c1):
        for c in range(c0, c1, 512):
            o = A(name, c, min(c + 512, c1))
            z = A("zz", 0, o[5])

            def fn(e, o=o, z=z):
                if e == "a":
                    return g.scalar.activation(o[0], z[0], AF.Copy)
                if e == "g":
                    return g.iota(o[0], [[0, o[5]]], 0, 0, allow_small_or_imprecise_dtypes=True)
                return g.vector.memset(o[0], 0.0)
            op("vag", {"v": cyc(o[5], True), "a": cyc(o[5]), "g": ("g", 0.13, 2 * o[5])}, fn, [z], [o])

    def gather(out, win, off, k0, k1, other=None, alu=None, ext=(), clamp=False):
        o, f = A(out, 16 * k0, 16 * k1), A(off[0], off[1] + k0, off[1] + k1)
        if other is None:
            def fn(e):
                if e == "a":
                    if clamp:
                        return g.scalar.activation(o[0], win[0].indirect(f[0]), AF.Relu, bias=15.0, scale=-1.0)
                    return g.scalar.activation(o[0], win[0].indirect(f[0]), AF.Copy)
                if clamp:
                    return g.vector.tensor_scalar(o[0], win[0].indirect(f[0]), 15.0, 15.0, ALU.min, ALU.subtract)
                return g.vector.tensor_copy(o[0], win[0].indirect(f[0]))
            return op("va", ("ga", o[5]), fn, [win, f], [o], ext=ext)
        b = A(other, 16 * k0, 16 * k1)
        return op("v", ("gt", o[5]), lambda e: g.vector.tensor_tensor(o[0], win[0].indirect(f[0]), b[0], alu), [win, f, b], [o], ext=ext)

    def mm(out, terms, start=True, stop=True, ext=(), pick=None):
        def fn(e):
            ins = None
            for i, (l, r) in enumerate(terms):
                lh = l[0] if pick is None else pick()
                ins = g.tensor.matmul(out[0], lh, r[0], start and i == 0, stop and i == len(terms) - 1)
            return ins
        return op("p", ("p", sum(max(64, r[5]) for l, r in terms)), fn, [x for t in terms for x in t], [out], ext=ext)

    def wq(v, q):
        return A("wv", WOFF[v] + 15 - q, WOFF[v] + 143 - q)

    def strided(v, buf, c0, c1):
        return [(wq(v, q), A(buf, c0 + q, c1, 16)) for q in range(16)]

    def blocks(v, buf, qs=range(16)):
        return [(wq(v, q), A(buf, M * q, M * (q + 1))) for q in qs]

    nb = [0]

    def bank(n=64):
        nb[0] += 1
        return A("ps%d" % nb[0], 0, n)

    def fold(terms, n=64):
        b = bank(n)
        mm(b, terms)
        return b

    def CH(name, j):
        return A(name, 64 * j, 64 * j + 64)

    def thirds(v, buf, extra=()):
        b = bank(M)
        for j in range(3):
            mm(CH(b[1], j), strided(v, buf, 1024 * j, 1024 * (j + 1)) + [(A(l), CH(x, j)) for l, x in extra])
        return b

    def quarters(v, buf):
        b = bank(M)
        for j in range(4):
            mm(b, blocks(v, buf, range(4 * j, 4 * j + 4)), j == 0, j == 3)
        return b

    def dma(out, in_, R, Wr, q="s", lat="row", ext=()):
        fn = lambda e: (g.sync if e == "s" else g.scalar).dma_start(out, in_)
        return op(q, ("d",), fn, R, Wr, lat=lat, kind="d", ext=ext)

    def torow(tabn, row, c0, src, q="s"):
        o = A(tabn, c0, c0 + 16 * src[5], row=row)
        return dma(o[0], src[0], [src], [o], q=q)

    def digits(h, l, x):
        aff(h, x)
        tt(l, x, h, ALU.subtract)

    def gp(fix, n, fn, R, Wr):
        return op("g", ("g", fix, 2 * n), fn, R, Wr)

    def gw(out, win, off, other=None, alu=None, ext=()):
        s = M // NCH
        for c in range(NCH):
            gather(out, win, (off, 0), s * c, s * (c + 1), other, alu, ext)

    for c0, src in ((PAI, T.par), (SDI, T.side), (HDI, T.heads)):
        a = A("ints", c0, c0 + (MI if c0 == HDI else M))
        dma(a[0], src[:], [], [a], q="sa", lat="small")
    for j in range(4):
        a = A("un", 768 * j, 768 * (j + 1))
        dma(a[0], T.cnt[:, 768 * j:768 * (j + 1)], [], [a], q="sa", lat="cnt%d" % j)
    for c0, src in ((ITI, T.itm), (BTI, T.bit)):
        a = A("ints", c0, c0 + M)
        dma(a[0], src[:], [], [a], q="sa", lat="late")
    dma(T.thi[:, 0:1], T.th[:], [], [A("thi")], q="sa", lat="late")

    mset(A("zz"), 0.0)
    mset(A("ones"), 1.0)
    gp(0.13, 1, lambda e: g.iota(T.pi[:, 0:1], [[0, 1]], 0, 1), [], [A("pi", 0, 1)])
    gp(0.13, M, lambda e: g.iota(T.mf[:], [[1, M]], 0, 0, allow_small_or_imprecise_dtypes=True), [], [A("mf")])
    zero("wv", 0, 144 * len(WV))
    zero("tab", 0, 2 * W)
    zero("pt", 0, W)
    for v, rows in WV.items():
        a = A("wv", WOFF[v] + 15, WOFF[v] + 143, 16)
        if rows is None:
            mset(a, 16384.0)
            gp(0.17, 8, lambda e, a=a: g.affine_select(a[0], a[0], [[-16, 8]], ALU.is_ge, 0.0, 0, 1), [a], [a])
            gp(0.17, 8, lambda e, a=a: g.affine_select(a[0], a[0], [[16, 8]], ALU.is_ge, 0.0, 15, -1), [a], [a])
        else:
            for r, w in rows.items():
                gp(0.17, 8, lambda e, a=a, r=r, w=w: g.affine_select(a[0], a[0], [[-16, 8]], ALU.not_equal, float(w), -r, 1), [a], [a])
    gp(0.17, 128, lambda e: g.affine_select(T.idn[:], T.ones[:], [[-1, 128]], ALU.is_equal, 0.0, 0, 1), [A("ones")], [A("idn")])
    gp(0.17, 128, lambda e: g.affine_select(T.bo[:], T.ones[:], [[-16, 8], [0, 16]], ALU.is_ge, 0.0, 0, 1), [A("ones")], [A("bo")])
    gp(0.17, 128, lambda e: g.affine_select(T.bo[:], T.bo[:], [[16, 8], [0, 16]], ALU.is_ge, 0.0, 15, -1), [A("bo")], [A("bo")])
    aff(A("nid"), A("idn"), -1.0)
    ts(A("pi", 1, 2), A("pi", 0, 1), 15, None, ALU.bitwise_and)
    cq, cq192, cq3, cnz, cz, cth, ck, csg, ctr, cd = [A("col", i, i + 1) for i in range(10)]
    aff(cq, A("pi", 1, 2))
    aff(cq192, cq, 192.0)
    aff(cq3, cq, 192.0, 3072.0)
    ts(cnz, cq, 0.5, None, ALU.is_ge)
    aff(cz, cnz, -float(KEPT), float(KEPT))
    ts(ck, cq, 3.5, None, ALU.is_lt)
    aff(csg, ck, 2.0, -1.0)
    aff(ctr, ck, 1.0, -0.5)
    aff(cd, ck, -1.0, 1.0)
    aff(cth, A("thi", 0, 1))
    if PRE[0] or PRE[1]:
        ts(A("col", 10, 11), cq, float(NX), 128.0, ALU.is_equal, ALU.mult)
        ts(A("f128"), A("bo"), A("col", 10, 11), None, ALU.mult)
    mset(A("one"), 1.0)
    mset(A("l3", W, W + 16), -1.0)
    for t in range(2):
        aff(A("kt%d" % t, I, I + 16), A("zz", 0, 16), 1.0, cd)
        aff(A("kt%d" % t, KEPT, KEPT + 1), ck)
    aff(A("idq"), A("zz", 0, M), 1.0, cq192)
    aff(A("idq3"), A("zz", 0, M), 1.0, cq3)
    aff(A("idm"), A("mf"))

    digits(A("hi", 0, ITI), A("lo", 0, ITI), A("ints", 0, ITI))
    for row, c0 in ((RB, PAI), (SD, SDI)):
        torow("tab", row, 0, A("hi", c0, c0 + M), "sa")
        torow("tab", row + 1, 0, A("lo", c0, c0 + M), "sa")
    for row, x in enumerate(("hi", "lo")):
        for h in range(NH):
            o, i = A("tab", W + I // NH * h, W + I // NH * (h + 1), row=row), A(x, HDI, HDI + MI)
            dma(o[0], T[x][h::NH, HDI:HDI + MI], [i], [o], q="sa")
    for row in (RA, RC):
        torow("tab", row, 0, A("idq"), "sa")
        torow("tab", row + 1, 0, A("idm"), "sa")
    aff(A("pa3"), A("ints", PAI, PAI + M), 1.0, 3072.0)
    aff(A("sdf"), A("ints", SDI, SDI + M))
    b = fold(strided("id", "tab", W, W + I))
    aff(A("ow", 0, MI), b)
    aff(A("hdf"), b)

    def nxt(pv, sdn, parts=((0, M),)):
        for c0, c1 in parts:
            xx, n0 = A(pv[1], M + c0, M + c1), bank(c1 - c0)
            tt(xx, A(pv[1], c0, c1), A("pa3", c0, c1), ALU.min)
            tt(n0, xx, A(sdn, c0, c1), ALU.max)
            digits(A("n0h", c0, c1), A("n0l", c0, c1), n0)
            digits(A("n1h", c0, c1), A("n1l", c0, c1), xx)
        torow("tab", NX, 0, A("n0h"), "sa")
        torow("tab", NX + 1, 0, A("n0l"), "sa")
        torow("tab", NX, W, A("n1h"), "sa")
        return torow("tab", NX + 1, W, A("n1l"), "sa")

    for h in range(2):
        gather("gu1", A("tab", 0, W), ("ow", 0), 32 * h, 32 * h + 32)
    aff(A("h3"), fold(strided("pa", "gu1", 0, I)), 1.0, 3072.0)
    aff(A("hs"), fold(strided("sd", "gu1", 0, I)))
    aff(A("osh"), fold(strided("sg", "gu1", 0, I)), 1.0, 0.25)
    ts(A("ints", ITI, ITI + 1), A("ints", ITI, ITI + 1), cnz, cz, ALU.mult, ALU.add)
    digits(A("hi", ITI, BTI), A("lo", ITI, BTI), A("ints", ITI, BTI))
    torow("tab", IT, 0, A("hi", ITI, BTI), "sa")
    torow("tab", IT + 1, 0, A("lo", ITI, BTI), "sa")
    aff(A("r1"), A("ints", BTI, BTI + M))
    aff(A("r0"), A("r1"), -1.0, 1.0)
    aff(A("nbf"), A("r0"))
    for r in ("r0", "r1"):
        ts(A(r, 0, 1), A(r, 0, 1), cnz, None, ALU.mult)
    torow("tab", R1, 0, A("r1"), "sa")
    torow("tab", R0, 0, A("r0"), "sa")

    pv = bank(M)
    for j in range(4):
        ge4(A("ge", 768 * j, 768 * (j + 1)), A("un", 768 * j, 768 * (j + 1)))
        mm(pv, blocks("vv", "ge", range(4 * j, 4 * j + 4)), j == 0, j == 3)
    ld = nxt(pv, "sdf")
    for j in range(2):
        a = A("uc", 1536 * j, 1536 * (j + 1))
        dma(a[0], T.cnt[:, a[2]:a[3]], [], [a], lat="big", ext=[ld])
    aff(A("opa"), thirds("pa", "tab"))
    b = thirds("sd", "tab")
    aff(A("osd"), b)
    aff(A("sdt"), b)
    tt(A("osc"), thirds("nsd", "tab", [("idn", "idq3"), ("idn", "idm")]), A("sdt"), ALU.max)

    others = [r for r in range(N) if r != rank]
    eng = topo.engines(core, T.cores[others[0]])

    def dst(r):
        a = topo.addr(T.cores[r])
        return DstId(rid=a[0], pnc=a[1])

    def remote(tr, src, kind, first):
        k = op("g", ("r",), lambda e: g.remote_dma_fused(tr, local_sem=T.sem.loc), [src], [], lat="first" if first else None, kind=kind)
        return op("w", ("w", 1.0 / NH), lambda e: None, [src], [], lat="fly", kind="w", ext=[k])

    def walk(t):
        acc = [bank(512), bank(512)]
        S = lambda n, s: A(n, MI * s, MI * (s + 1))
        for s in range(4):
            gwn = "gw%d" % (s % 2)
            for h in range(2):
                gather(gwn, A("ge") if s == 0 else A("tab"), ("ow", MI * s), 32 * h, 32 * h + 32)
            if s == 0:
                b = fold(strided("vv", gwn, 0, I))
                pn, prev = A(b[1], 128, 192), A("hs")
                tt(pn, b, A("h3"), ALU.min)
            else:
                pn, prev = fold(strided("nx", gwn, 0, I)), S("sck", s - 1)
            nf = A(pn[1], 64, 128)
            if s < 3:
                tt(S("ow", s + 1), pn, prev, ALU.max)
                tt(S("wf", s), pn, prev, ALU.max)
            ts(nf, pn, 3072.0, 3072.0, ALU.is_ge, ALU.mult)
            if s == 0:
                tt(S("sck", 0), nf, A("hs"), ALU.min)
            elif s == 1:
                tt(S("sc", 1), fold(strided("sd", gwn, 0, I)), S("sck", 0), ALU.add)
                tt(S("sck", 1), nf, S("sc", 1), ALU.min)
            tt(S("om", s), A("hdf") if s == 0 else S("wn", s - 1), nf, ALU.min)
            if s < 3:
                tt(S("wn", s), S("wf", s), nf, ALU.subtract)
            for h in range(2):
                k = gather("gu%d" % s, A("un"), ("om", MI * s), 32 * h, 32 * h + 32, clamp=t == 1)
                pick = (lambda k=k: T.nid[:] if where[k] == "a" else T.idn[:]) if t == 1 else None
                mm(acc[h], [(A("nid" if t == 1 else "idn"), A("gu%d" % s, 512 * h, 512 * h + 512))], s == 0, s == 3, pick=pick)
        snd, lnd, kt = "snd%d" % t, "lnd%d" % t, "kt%d" % t
        mask = 0
        for e_ in eng:
            mask |= 1 << e_
        for h in range(2):
            aff(A(snd, 512 * h, 512 * h + 512), acc[h], 1.0, 60.0 * t)
        n, kv = 128 // NH, []
        for h in range(NH):
            c = I // NH * h
            tr = [RemoteDMATransfer(dst_ids=[dst(r)], dma_engine_mask=1 << eng[i], remote_sem=T.sem["rs%d%d" % (t, h)],
                                    src=T[snd][:, c + n * r:c + n * (r + 1)], dst=T[lnd][:, c + n * rank:c + n * (rank + 1)])
                  for i, r in enumerate(others)]
            k1 = remote(tr, A(snd, c, c + I // NH), ("rs%d%d" % (t, h), N - 1, N - 1), t + h == 0)
            tot = bank(n)
            mm(tot, [(A("idn"), A(snd if r == rank else lnd, c + n * r, c + n * (r + 1))) for r in range(N)], ext=[k1])
            ts(A("gev", n * h, n * h + n), tot, cth, 0.5, ALU.is_ge, ALU.subtract)
            pc = fold([(A("bo"), A("gev", n * h, n * h + n))], n)
            own = A(kt, 128 * rank + n * h, 128 * rank + n * h + n)
            ts(own, pc, csg, ctr, ALU.mult, ALU.is_ge)
            tr = [RemoteDMATransfer(dst_ids=[dst(r) for r in others], dma_engine_mask=mask, remote_sem=T.sem["kv%d%d" % (t, h)],
                                    srcs=[own[0]], dsts=[own[0] for r in others])]
            kv.append(remote(tr, own, ("kv%d%d" % (t, h), (N - 1) * len(eng), len(eng)), False))
            aff(A("yas", 128 * t + n * h, 128 * t + n * h + n), tot)
        return kv

    def pre_par(t):
        gw("ga", A("tab", 0, W), "opa")
        aff(A("oip"), thirds("it", "ga"))
        for r in range(2):
            o, i = A("ga", row=RE + r), A("tab", 0, W, row=RA + r)
            dma(o[0], i[0], [i], [o], q="sa")
        torow("ga", NX, 0, A("one"), "sa")
        if PRE[t]:
            gw("sm", A("un"), "opa", "uc", ALU.add)

    def partners(t):
        ca = bank(M)
        for j in range(3):
            mm(CH(ca[1], j), strided("itb%d" % t, "tab", 1024 * j, 1024 * (j + 1)) + strided("r%dn" % (1 - t), "gb", 1024 * j, 1024 * (j + 1)))
        ts(A("t1"), ca, BIG * (1 + t), float(DROP), ALU.add, ALU.min)
        cs = thirds("itr%d" % t, "pt", [("idn", "pb%d" % (1 - t))])
        tt(A("oit0" if t == 0 else "o1f"), cs, A("t1"), ALU.min)
        b = thirds("id", "pt", [("nid", "pen%d" % (1 - t))])
        tt(A("op%d" % t), b, A("sa%d" % t), ALU.max)
        if t == 1:
            aff(A("ox"), b)

    def pre_side():
        win = A("pt")
        for c in range(W // SCH):
            src, f = A("tab", SCH * c, SCH * c + SCH), A("osc", SCH // 16 * c, SCH // 16 * (c + 1))
            op("v", ("sc", SCH), lambda e, src=src, f=f: g.vector.tensor_copy(win[0].indirect(f[0]), src[0]), [src, f], [win])
        gw("gb", A("tab", 0, W), "osd")
        b = thirds("bit", "tab")
        aff(A("pen0"), b, BIG)
        aff(A("pen1"), b, -BIG, BIG)
        aff(A("pb0"), b, BIG, BIG)
        aff(A("pb1"), b, -BIG, 2 * BIG)
        for t in range(2):
            tt(A("sa%d" % t), A("sdt"), A("pen%d" % t), ALU.subtract)
        partners(0)
        for x, v, own in (("dq", "a0", "idq"), ("dm", "a1", "idm")):
            b = bank(M)
            mm(b, [(A("nid"), A(own))], True, False)
            for j in range(4):
                mm(b, blocks(v, "pt", range(4 * j, 4 * j + 4)), False, j == 3)
            for t in range(2):
                tt(A("%s%d" % (x, t)), b, A("r%d" % (1 - t)), ALU.mult)
        b = quarters("sd", "gb")
        tt(A(b[1], M, 2 * M), b, A("nbf"), ALU.mult)
        tt(A("ds"), A(b[1], M, 2 * M), A("sdf"), ALU.subtract)

    def post(t, kv):
        kt = A("kt%d" % t)
        gw("a1", kt, "oip", "ga", ALU.mult, ext=kv)
        gw("k0", kt, "oit%d" % t, ext=kv)
        for j in range(3):
            if PRE[t]:
                aff(CH("o2", j), fold(strided("nxs", "a1", 1024 * j, 1024 * (j + 1))))
                continue
            b = fold(strided("nxd", "a1", 1024 * j, 1024 * (j + 1)))
            ts(CH("t3", j), b, 4096.0, -4096.0, ALU.is_ge, ALU.mult)
            tt(CH("o2", j), b, CH("t3", j), ALU.add)
            aff(CH("opm", j), b, 1.0, -4096.0)
        tt(A("opk"), thirds("kd", "k0"), A("op%d" % t), ALU.max)
        gw("l2", A("a1"), "o2")
        if PRE[t]:
            for c in range(6):
                b = fold([(A("idn"), A("un", 512 * c, 512 * c + 512)), (A("f128"), A("a1", 512 * c, 512 * c + 512))], 512)
                tt(A("ua", 512 * c, 512 * c + 512), b, A("sm", 512 * c, 512 * c + 512), ALU.min)
        else:
            gw("ua", A("un"), "opm", "uc", ALU.add)
        for c in range(G6A[t], 6):
            o, i = A("ub", 512 * c, 512 * c + 512), A("ua", 512 * c, 512 * c + 512)
            dma(o[0], i[0], [i], [o], lat="out")
        for j in range(3):
            aff(CH("o3", j), fold(strided("nxs", "l2", 1024 * j, 1024 * (j + 1))))
        gw("l3", A("l2"), "o3")
        bt = [bank() for j in range(3)]
        for j in range(3):
            mm(bt[j], strided("nval", "l3", 1024 * j, 1024 * (j + 1)), True, False)
        b = quarters("val", "l3")
        aff(A("p1f"), b)
        aff(A("oi"), b)
        gw("g5", A("l3"), "opk")
        b = quarters("val", "g5")
        hit = A(b[1], M, 2 * M)
        tt(hit, b, A("p1f"), ALU.is_equal)
        tt(A("deh"), hit, A("dq%d" % t), ALU.mult)
        tt(A("del"), hit, A("dm%d" % t), ALU.mult)
        torow("tab", RE, 0, A("deh"), "sa")
        torow("tab", RE + 1, 0, A("del"), "sa")
        for j in range(3):
            mm(bt[j], strided("val", "g5", 1024 * j, 1024 * (j + 1)), False, True)
            hb = A(bt[j][1], 64, 128)
            ts(hb, bt[j], 0.0, BIG, ALU.is_equal, ALU.mult)
            tt(CH("osm", j), hb, CH("sa%d" % t, j), ALU.min)
            if t == 0:
                tt(CH("sa1", j), CH("sa1", j), hb, ALU.subtract)
        if t == 0:
            b = bank(M)
            tt(b, hit, A("ds"), ALU.mult)
            aff(A("hit"), hit)
            torow("tab", R0, 0, A("hit"), "sa")
            tt(A("sd1"), b, A("sdf"), ALU.add)
            digits(A("sdh"), A("sdl"), A("sd1"))
            torow("tab", SD, 0, A("sdh"), "sa")
            torow("tab", SD + 1, 0, A("sdl"), "sa")
        pv = bank(M) if t == 0 else None
        for c in range(6):
            a = A("un", 512 * c, 512 * (c + 1))
            if c >= G6A[t]:
                gather("un", A("ua"), ("osm", 0), 32 * c, 32 * c + 32, "ub", ALU.add)
                if t == 1:
                    ts(a, a, 15.0, None, ALU.min)
                    dma(T.yc[:, a[2]:a[3]], a[0], [a], [], lat="out")
                continue
            gather("g6", A("ua"), ("osm", 0), 32 * c, 32 * c + 32)
            b = fold([(A("idn"), A(x, a[2], a[3])) for x in ("ua", "g6")], 512)
            if t == 0:
                aff(a, b)
            else:
                ts(a, b, 15.0, None, ALU.min)
                dma(T.yc[:, a[2]:a[3]], a[0], [a], [], lat="out")
        if t == 0:
            for j in range(4):
                ge4(A("ge", 768 * j, 768 * (j + 1)), A("un", 768 * j, 768 * (j + 1)))
                mm(pv, blocks("vv", "ge", range(4 * j, 4 * j + 4)), j == 0, j == 3)
            for h in range(2):
                gather("gu1", A("tab", 0, W), ("ow", 0), 32 * h, 32 * h + 32)
            aff(A("hs"), fold(strided("sd", "gu1", 0, I)))
        gw("g7", A("tab", 0, W), "oi")
        for j in range(3):
            b = fold(strided("rp", "g7", 1024 * j, 1024 * (j + 1)))
            if t == 0:
                aff(CH("pa3", j), b, 1.0, 3072.0)
                digits(CH("pah", j), CH("pal", j), b)
            else:
                aff(CH("ypf", j), b)
        if t == 0:
            for h in range(2):
                gather("gu2", A("g7"), ("osh", 0), 32 * h, 32 * h + 32)
            aff(A("h3"), fold(strided("rp", "gu2", 0, I)), 1.0, 3072.0)
            nxt(pv, "sd1", ((0, 128), (128, M)))
            torow("tab", RB, 0, A("pah"), "sa")
            ld = torow("tab", RB + 1, 0, A("pal"), "sa")
            for j in range(2):
                o, i = A("uc", 1536 * j, 1536 * (j + 1)), A("un", 1536 * j, 1536 * (j + 1))
                dma(o[0], i[0], [i], [o], lat="big", ext=[ld])
        else:
            dma(T.yp[:], T.ypf[:], [A("ypf")], [], q="sa")

    kv = walk(0)
    pre_par(0)
    pre_side()
    post(0, kv)
    kv = walk(1)
    dma(T.ya[:], T.yas[:], [A("yas")], [])
    aff(A("opa"), thirds("pa", "tab"))
    partners(1)
    pre_par(1)
    gw("g5", A("tab", 0, W), "ox")
    tt(A("oit1"), thirds("h", "g5"), A("o1f"), ALU.max)
    post(1, kv)
    return ops


def plan(ops):
    order = [(int(w[:-1], 16), w[-1]) for w in ORDER.split()]
    assert sorted(k for k, _ in order) == list(range(len(ops)))
    return order


def banks(ops, order):
    users = {}
    for i, (k, _) in enumerate(order):
        for b in ops[k]["banks"]:
            users.setdefault(b, []).append((i, k))
    place, extra = {}, {}
    tenant = [None] * 8
    for i, (k, _) in enumerate(order):
        for b in ops[k]["banks"]:
            if b not in place:
                last = [users[x][-1][0] if x else -1 for x in tenant]
                p = last.index(min(last))
                if last[p] >= i:
                    return None, None
                extra.setdefault(k, []).extend(j for _, j in users.get(tenant[p], []))
                tenant[p] = b
                place[b] = p
    return place, extra


def rank_program(g, core, T, topo):
    rank = T.rank_of(core)
    if rank is None:
        return
    ops = build(g, T, topo, core, rank)
    order = plan(ops)
    place, extra = banks(ops, order)
    ops = build(g, T, topo, core, rank, place)
    for k, js in extra.items():
        for j in js:
            ops[k]["deps"][j] = True
    queue = {"v": g.vector, "a": g.scalar, "p": g.tensor, "s": g.sync, "g": g}
    count = {"cv": 0, "ca": 0, "cp": 0, "cg": 0, "loc": 0}
    done, where = {}, {}
    seen = {e: {} for e in queue}
    nd = 0
    for k, e in order:
        o = ops[k]
        assert e in o["engs"]
        if e == "w":
            where[k], done[k] = e, done[max(o["deps"])]
            continue
        need = {}
        for j, hard in o["deps"].items():
            if where[j] == e and ops[j]["kind"] == "c" and o["kind"] == "c" and (e == "p" or not hard):
                continue
            s, v = done[j]
            need[s] = max(need.get(s, 0), v)
        for s, v in need.items():
            if seen[e].get(s, 0) < v:
                queue[e].wait_ge(T.sem[s], v)
                seen[e][s] = v
        ins = o["fn"](e)
        where[k] = e
        if o["kind"] == "c":
            s = "c" + e
            count[s] += 1
            ins.then_inc(T.sem[s], 1)
            done[k] = (s, count[s])
        elif o["kind"] == "d":
            s = "d%d" % nd
            nd += 1
            ins.then_inc(T.sem[s], 16)
            count[s] = 16
            done[k] = (s, 16)
        else:
            s, v, loc = o["kind"]
            count[s] = v
            count["loc"] += loc
            done[k] = (s, v)
    for s, v in count.items():
        if v > 0 and max(seen[e].get(s, 0) for e in seen) < v:
            g.wait_ge(T.sem[s], v)
